import numpy as np
import ml_dtypes


def mxq(x, axis, fmt="e4m3"):
    dtype, down = {"e4m3": (ml_dtypes.float8_e4m3fn, 7), "e5m2": (ml_dtypes.float8_e5m2, 14)}[fmt]
    v = np.moveaxis(np.asarray(x, np.float32).astype(ml_dtypes.bfloat16).astype(np.float64), axis, -1)
    blocks = v.reshape(v.shape[:-1] + (-1, 32))
    amax = np.abs(blocks).max(-1, keepdims=True)
    byte = np.maximum(np.where(amax > 0, np.frexp(amax)[1] - 1 + 127, 0) - down, 1)
    scale = np.exp2(byte - 127.0)
    codes = (blocks / scale).astype(np.float32).astype(dtype).astype(np.float64)
    return np.moveaxis((codes * scale).reshape(v.shape), -1, axis)


WIDE = False


def mx_kscale(k):
    if not WIDE:
        return np.ones(k)
    levels = np.array([10, -10, 5, -5, 0])
    if k % 512:
        return np.exp2(np.random.permutation(np.resize(levels, k // 32))).repeat(32)
    a = np.empty((k // 512, 16))
    for p in range(k // 512):
        a[p, :8] = np.random.permutation(np.resize(levels, 8))
        for g in range(8):
            far = levels[np.abs(levels - a[p, g]) >= 10]
            a[p, g + 8] = far[np.random.randint(len(far))]
    return np.exp2(a.ravel()).repeat(32)


def f64(x):
    return np.asarray(x).astype(np.float64)


def striped(idx):
    return np.tile(idx.reshape(-1, 16).T, (8, 1)).astype(np.uint16)


def unstriped(offs):
    return offs[:16].T.reshape(-1).astype(np.int64)


def pack_weight(w):
    k, n = w.shape
    w = f64(np.asarray(w, np.float32).astype(ml_dtypes.bfloat16)).reshape(k // 32, 32, n)
    amax = np.abs(w).max(1)
    byte = np.clip(np.where(amax > 0, np.frexp(amax)[1] - 1 + 127 - 7, 1), 1, 254)
    scaled = (w * np.exp2(127.0 - byte)[:, None, :]).reshape(k, n).astype(np.float32)
    words = np.ascontiguousarray(scaled.reshape(k // 512, 128, 4, n).transpose(0, 1, 3, 2)).astype(ml_dtypes.float8_e4m3fn).view(np.uint8)
    return words, np.ascontiguousarray(byte.astype(np.uint8).reshape(k // 512, 16, n))


def unpack_weight(words, scales):
    g, p, n, _ = words.shape
    vals = np.ascontiguousarray(words).view(ml_dtypes.float8_e4m3fn).astype(np.float64) * np.repeat(np.exp2(scales.astype(np.float64) - 127.0), 8, axis=1)[..., None]
    return vals.transpose(0, 1, 3, 2).reshape(g * 512, n)


K, T, S, N = 1024, 1024, 512, 256


def setup_inputs():
    n = np.random.standard_normal
    s = mx_kscale(K)[:, None]
    words, scales = pack_weight(n((K, N)) / np.sqrt(K) / s)
    return {
        "xT": (n((K, S)) * s).astype(np.float32),
        "w_words": words,
        "w_scales": scales,
        "gate": np.tile(np.random.uniform(0.2, 1.0, S), (N, 1)).astype(np.float32),
        "offs": striped(np.random.permutation(T)[:S]),
    }


def reference(xT, w_words, w_scales, gate, offs):
    w = unpack_weight(w_words, w_scales)
    idx = unstriped(offs)
    xq = mxq(f64(xT), 0, "e4m3")
    y = w.T @ xq
    out = np.zeros((N, T))
    out[:, idx] = f64(gate) * y
    return out

@@ -1,0 +1,155 @@
+from contextlib import ExitStack
+
+import concourse.mybir as mybir
+
+K, T, S, N = 1024, 1024, 512, 256
+FLOPS = 2 * K * S * N
+
+F32 = mybir.dt.float32
+BF16 = mybir.dt.bfloat16
+I32 = mybir.dt.int32
+U32 = mybir.dt.uint32
+U16 = mybir.dt.uint16
+U8 = mybir.dt.uint8
+FP8X4 = mybir.dt.float8_e4m3fn_x4
+MULT = mybir.AluOpType.mult
+
+P = 128
+PACK = 4
+PASSES = K // (P * PACK)
+M_TILES = N // P
+W = 128
+CHUNKS = S // W
+RUN = 4
+X_LOADS = [(0, 0, 2), (1, 0, 1), (1, 1, 2), (0, 2, 4), (1, 2, 3), (1, 3, 4)]
+GATE_CUTS = [(0, 256), (256, 512)]
+
+
+def tile_picked_place_lin_none_sub_l_kernel(tc, xT, w_words, w_scales, gate, offs, out):
+    nc = tc.nc
+    x_rows = xT.rearrange("(a p t) j -> a p t j", a=PASSES, t=PACK)
+    w_rows = w_words.rearrange("a p m r -> p a (m r)").bitcast(I32)
+    scale_rows = w_scales.rearrange("a (q i) m -> i q a m", i=4).bitcast(I32)
+    gate_rows = gate.rearrange("(h p) j -> p h j", p=P)
+
+    with ExitStack() as ctx:
+        keep = ctx.enter_context(tc.tile_pool(name="keep", bufs=1))
+        psum = ctx.enter_context(tc.psum_pool(name="psum", bufs=1))
+
+        offsets = keep.tile([P, S // 16], U16, name="offsets")
+        w_codes = keep.tile([P, PASSES, N], U32, name="w_codes", align_bytes=64)
+        w_planes = keep.tile([P, PASSES, N], U8, name="w_planes", align_bytes=64)
+        gates = [keep.tile([P, M_TILES, hi - lo], F32, name=f"gates{lo}") for lo, hi in GATE_CUTS]
+        spark = keep.tile([P, 1], F32, name="spark")
+        sparked = keep.tile([P, 1], F32, name="sparked")
+        windows = [keep.tile([P, T], F32, name=f"window{h}") for h in range(M_TILES)]
+        raws = []
+        raw_of = {}
+        for n, (a, lo, hi) in enumerate(X_LOADS):
+            raws.append(keep.tile([P, PACK, (hi - lo) * W], F32, name=f"raw{n}"))
+            for c in range(lo, hi):
+                raw_of[c, a] = raws[n][:, :, (c - lo) * W : (c - lo + 1) * W]
+        grouped = [keep.tile([P, PASSES, W * PACK], BF16, name=f"grouped{c}", align_bytes=64) for c in range(CHUNKS)]
+        codes = [keep.tile([P, PASSES, W], U32, name=f"codes{c}", align_bytes=64) for c in range(CHUNKS)]
+        planes = [keep.tile([P, PASSES, W], U8, name=f"planes{c}", align_bytes=64) for c in range(CHUNKS)]
+        banks = [[psum.tile([P, W], F32, name=f"bank{c}_{h}") for h in range(M_TILES)] for c in range(CHUNKS)]
+        sums = [[keep.tile([P, W], F32, name=f"sums{c}_{h}") for h in range(M_TILES)] for c in range(CHUNKS)]
+
+        nc.vector.memset(w_planes[:].rearrange("p a m -> p (a m)").bitcast(I32), 0)
+        nc.vector.memset(spark[:], 0.0)
+        nc.scalar.copy(sparked[:], spark[:])
+
+        def load_x(n):
+            a, lo, hi = X_LOADS[n]
+            nc.sync.dma_start(raws[n][:], x_rows[a][:, :, lo * W : hi * W])
+
+        def load_gate(u, queue):
+            lo, hi = GATE_CUTS[u]
+            queue.dma_start(gates[u][:], gate_rows[:, :, lo:hi])
+
+        load_x(0)
+        load_x(1)
+        nc.sync.dma_start(w_codes[:].bitcast(I32), w_rows)
+        for i in range(4):
+            nc.sync.dma_start(w_planes[i:P:32, :, :].bitcast(I32), scale_rows[i])
+        load_x(2)
+        nc.sync.dma_start(offsets[:], offs)
+        for u in range(2):
+            load_gate(u, nc.gpsimd)
+        for n in range(3, len(X_LOADS)):
+            load_x(n)
+        for h in range(M_TILES):
+            nc.vector.memset(windows[h][:], 0.0)
+
+        def pack(c, a):
+            dst = grouped[c][:, a, :].rearrange("p (c i t) -> p c t i", i=RUN, t=PACK)
+            src = raw_of[c, a].rearrange("p t (c i) -> p c t i", i=RUN)
+            if (c, a) in [(0, 0), (0, 1), (1, 1)]:
+                nc.vector.tensor_copy(dst, src)
+            else:
+                nc.scalar.copy(dst, src)
+
+        def quantize(c, a):
+            nc.vector.quantize_mx(out=codes[c][:, a, :].bitcast(FP8X4), scales=planes[c][:, a, :], in_=grouped[c][:, a, :])
+
+        def quantize_both(c):
+            nc.vector.quantize_mx(
+                out=codes[c][:].rearrange("p a w -> p (a w)").bitcast(FP8X4),
+                scales=planes[c][:].rearrange("p a w -> p (a w)"),
+                in_=grouped[c][:].rearrange("p a w -> p (a w)"),
+            )
+
+        def multiply(c):
+            for h in range(M_TILES):
+                cols = slice(h * P, (h + 1) * P)
+                for a in range(PASSES):
+                    nc.tensor.matmul_mx(
+                        out=banks[c][h][:],
+                        lhsT=w_codes[:, a, cols].bitcast(FP8X4),
+                        lhsT_scale=w_planes[:, a, cols],
+                        rhs=codes[c][:, a, :].bitcast(FP8X4),
+                        rhs_scale=planes[c][:, a, :],
+                        start=(a == 0),
+                        stop=(a == PASSES - 1),
+                    )
+                nc.scalar.copy(sums[c][h][:], banks[c][h][:])
+
+        def scatter(c, h):
+            places = offsets[:, c * (W // 16) : (c + 1) * (W // 16)]
+            u = c // 2
+            j0 = c * W - GATE_CUTS[u][0]
+            nc.vector.tensor_tensor(
+                windows[h][:].indirect(places), sums[c][h][:], gates[u][:, h, j0 : j0 + W], MULT
+            )
+
+        def store(h):
+            nc.sync.dma_start(out[h * P : (h + 1) * P, :], windows[h][:])
+
+        pack(0, 0)
+        quantize(0, 0)
+        pack(1, 0)
+        pack(0, 1)
+        quantize(0, 1)
+        multiply(0)
+        quantize(1, 0)
+        pack(1, 1)
+        quantize(1, 1)
+        scatter(0, 0)
+        multiply(1)
+        scatter(0, 1)
+        scatter(1, 0)
+        for a in range(PASSES):
+            pack(2, a)
+        quantize_both(2)
+        multiply(2)
+        scatter(1, 1)
+        for a in range(PASSES):
+            pack(3, a)
+        quantize_both(3)
+        multiply(3)
+        scatter(2, 0)
+        scatter(3, 0)
+        store(0)
+        scatter(2, 1)
+        scatter(3, 1)
+        store(1)

@@ -21,16 +21,13 @@ M_TILES = N // P
 W = 128
 CHUNKS = S // W
 RUN = 4
-X_LOADS = [(0, 0, 2), (1, 0, 1), (1, 1, 2), (0, 2, 4), (1, 2, 3), (1, 3, 4)]
-GATE_CUTS = [(0, 256), (256, 512)]
 
 
 def tile_picked_place_lin_none_sub_l_kernel(tc, xT, w_words, w_scales, gate, offs, out):
     nc = tc.nc
     x_rows = xT.rearrange("(a p t) j -> a p t j", a=PASSES, t=PACK)
     w_rows = w_words.rearrange("a p m r -> p a (m r)").bitcast(I32)
-    scale_rows = w_scales.rearrange("a (q i) m -> i q a m", i=4).bitcast(I32)
-    gate_rows = gate.rearrange("(h p) j -> p h j", p=P)
+    scale_rows = w_scales.rearrange("a (q i) m -> q a i m", i=4).bitcast(I32)
 
     with ExitStack() as ctx:
         keep = ctx.enter_context(tc.tile_pool(name="keep", bufs=1))
@@ -38,53 +35,50 @@ def tile_picked_place_lin_none_sub_l_kernel(tc, xT, w_words, w_scales, gate, off
 
         offsets = keep.tile([P, S // 16], U16, name="offsets")
         w_codes = keep.tile([P, PASSES, N], U32, name="w_codes", align_bytes=64)
-        w_planes = keep.tile([P, PASSES, N], U8, name="w_planes", align_bytes=64)
-        gates = [keep.tile([P, M_TILES, hi - lo], F32, name=f"gates{lo}") for lo, hi in GATE_CUTS]
+        w_planes = keep.tile([P, N], U8, name="w_planes", align_bytes=64)
         spark = keep.tile([P, 1], F32, name="spark")
         sparked = keep.tile([P, 1], F32, name="sparked")
         windows = [keep.tile([P, T], F32, name=f"window{h}") for h in range(M_TILES)]
-        raws = []
-        raw_of = {}
-        for n, (a, lo, hi) in enumerate(X_LOADS):
-            raws.append(keep.tile([P, PACK, (hi - lo) * W], F32, name=f"raw{n}"))
-            for c in range(lo, hi):
-                raw_of[c, a] = raws[n][:, :, (c - lo) * W : (c - lo + 1) * W]
         grouped = [keep.tile([P, PASSES, W * PACK], BF16, name=f"grouped{c}", align_bytes=64) for c in range(CHUNKS)]
         codes = [keep.tile([P, PASSES, W], U32, name=f"codes{c}", align_bytes=64) for c in range(CHUNKS)]
         planes = [keep.tile([P, PASSES, W], U8, name=f"planes{c}", align_bytes=64) for c in range(CHUNKS)]
+        raws = [[keep.tile([P, PACK, W], F32, name=f"raw{c}_{a}") for a in range(PASSES)] for c in range(CHUNKS)]
+        gate_first = keep.tile([P, W], F32, name="gate_first")
+        gate_rest = keep.tile([P, S - W], F32, name="gate_rest")
+        gates = [gate_first[:]] + [gate_rest[:, c * W : (c + 1) * W] for c in range(CHUNKS - 1)]
         banks = [[psum.tile([P, W], F32, name=f"bank{c}_{h}") for h in range(M_TILES)] for c in range(CHUNKS)]
-        sums = [[keep.tile([P, W], F32, name=f"sums{c}_{h}") for h in range(M_TILES)] for c in range(CHUNKS)]
+        sums = [[keep.tile([P, W], F32, name=f"sums{c}_{h}")[:] if (c, h) not in [(0, 1), (1, 0), (1, 1), (2, 0), (2, 1)] else None for h in range(M_TILES)] for c in range(CHUNKS)]
+        sums[0][1] = raws[1][1][:, 0, :]
+        for c in (1, 2):
+            for h in range(M_TILES):
+                sums[c][h] = raws[c + 1][1][:, h, :]
 
-        nc.vector.memset(w_planes[:].rearrange("p a m -> p (a m)").bitcast(I32), 0)
+        nc.vector.memset(w_planes[:].bitcast(I32), 0)
         nc.vector.memset(spark[:], 0.0)
         nc.scalar.copy(sparked[:], spark[:])
 
-        def load_x(n):
-            a, lo, hi = X_LOADS[n]
-            nc.sync.dma_start(raws[n][:], x_rows[a][:, :, lo * W : hi * W])
+        def load_x(c, a):
+            nc.sync.dma_start(raws[c][a][:], x_rows[a][:, :, c * W : (c + 1) * W])
 
-        def load_gate(u, queue):
-            lo, hi = GATE_CUTS[u]
-            queue.dma_start(gates[u][:], gate_rows[:, :, lo:hi])
-
-        load_x(0)
-        load_x(1)
-        nc.sync.dma_start(w_codes[:].bitcast(I32), w_rows)
-        for i in range(4):
-            nc.sync.dma_start(w_planes[i:P:32, :, :].bitcast(I32), scale_rows[i])
-        load_x(2)
         nc.sync.dma_start(offsets[:], offs)
-        for u in range(2):
-            load_gate(u, nc.gpsimd)
-        for n in range(3, len(X_LOADS)):
-            load_x(n)
+        load_x(0, 0)
+        load_x(0, 1)
+        nc.sync.dma_start(w_codes[:].bitcast(I32), w_rows)
+        for q in range(4):
+            nc.sync.dma_start(w_planes[32 * q : 32 * q + 4 * PASSES, :].bitcast(I32), scale_rows[q])
+        nc.gpsimd.dma_start(gate_first[:], gate[0:P, 0:W])
+        for c in range(1, CHUNKS):
+            for a in range(PASSES):
+                load_x(c, a)
+            if c == 2:
+                nc.sync.dma_start(gate_rest[:], gate[0:P, W:S])
         for h in range(M_TILES):
             nc.vector.memset(windows[h][:], 0.0)
 
         def pack(c, a):
             dst = grouped[c][:, a, :].rearrange("p (c i t) -> p c t i", i=RUN, t=PACK)
-            src = raw_of[c, a].rearrange("p t (c i) -> p c t i", i=RUN)
-            if (c, a) in [(0, 0), (0, 1), (1, 1)]:
+            src = raws[c][a][:].rearrange("p t (c i) -> p c t i", i=RUN)
+            if (c, a) == (0, 1):
                 nc.vector.tensor_copy(dst, src)
             else:
                 nc.scalar.copy(dst, src)
@@ -92,64 +86,53 @@ def tile_picked_place_lin_none_sub_l_kernel(tc, xT, w_words, w_scales, gate, off
         def quantize(c, a):
             nc.vector.quantize_mx(out=codes[c][:, a, :].bitcast(FP8X4), scales=planes[c][:, a, :], in_=grouped[c][:, a, :])
 
-        def quantize_both(c):
-            nc.vector.quantize_mx(
-                out=codes[c][:].rearrange("p a w -> p (a w)").bitcast(FP8X4),
-                scales=planes[c][:].rearrange("p a w -> p (a w)"),
-                in_=grouped[c][:].rearrange("p a w -> p (a w)"),
-            )
+        def multiply(c, h):
+            cols = slice(h * P, (h + 1) * P)
+            for a in range(PASSES):
+                nc.tensor.matmul_mx(
+                    out=banks[c][h][:],
+                    lhsT=w_codes[:, a, cols].bitcast(FP8X4),
+                    lhsT_scale=w_planes[4 * a : P, cols],
+                    rhs=codes[c][:, a, :].bitcast(FP8X4),
+                    rhs_scale=planes[c][:, a, :],
+                    start=(a == 0),
+                    stop=(a == PASSES - 1),
+                )
 
-        def multiply(c):
-            for h in range(M_TILES):
-                cols = slice(h * P, (h + 1) * P)
-                for a in range(PASSES):
-                    nc.tensor.matmul_mx(
-                        out=banks[c][h][:],
-                        lhsT=w_codes[:, a, cols].bitcast(FP8X4),
-                        lhsT_scale=w_planes[:, a, cols],
-                        rhs=codes[c][:, a, :].bitcast(FP8X4),
-                        rhs_scale=planes[c][:, a, :],
-                        start=(a == 0),
-                        stop=(a == PASSES - 1),
-                    )
-                nc.scalar.copy(sums[c][h][:], banks[c][h][:])
+        def unload(c, h):
+            if (c, h) == (0, 0):
+                nc.vector.tensor_copy(sums[c][h], banks[c][h][:])
+            else:
+                nc.scalar.copy(sums[c][h], banks[c][h][:])
 
         def scatter(c, h):
             places = offsets[:, c * (W // 16) : (c + 1) * (W // 16)]
-            u = c // 2
-            j0 = c * W - GATE_CUTS[u][0]
-            nc.vector.tensor_tensor(
-                windows[h][:].indirect(places), sums[c][h][:], gates[u][:, h, j0 : j0 + W], MULT
-            )
+            nc.vector.tensor_tensor(windows[h][:].indirect(places), sums[c][h], gates[c], MULT)
 
-        def store(h):
-            nc.sync.dma_start(out[h * P : (h + 1) * P, :], windows[h][:])
+        def prepare(c):
+            for a in range(PASSES):
+                pack(c, a)
+            for a in range(PASSES):
+                quantize(c, a)
 
-        pack(0, 0)
-        quantize(0, 0)
-        pack(1, 0)
-        pack(0, 1)
-        quantize(0, 1)
-        multiply(0)
-        quantize(1, 0)
-        pack(1, 1)
-        quantize(1, 1)
-        scatter(0, 0)
-        multiply(1)
-        scatter(0, 1)
-        scatter(1, 0)
-        for a in range(PASSES):
-            pack(2, a)
-        quantize_both(2)
-        multiply(2)
-        scatter(1, 1)
-        for a in range(PASSES):
-            pack(3, a)
-        quantize_both(3)
-        multiply(3)
-        scatter(2, 0)
-        scatter(3, 0)
-        store(0)
-        scatter(2, 1)
-        scatter(3, 1)
-        store(1)
+        def finish(c, h):
+            unload(c, h)
+            scatter(c, h)
+
+        def products(c):
+            prepare(c)
+            for h in range(M_TILES):
+                multiply(c, h)
+
+        products(0)
+        finish(0, 0)
+        products(1)
+        finish(0, 1)
+        for c in range(1, CHUNKS):
+            if c + 1 < CHUNKS:
+                products(c + 1)
+            finish(c, 0)
+            if c + 1 == CHUNKS:
+                nc.sync.dma_start(out[0:P, :], windows[0][:])
+            finish(c, 1)
+        nc.sync.dma_start(out[P : 2 * P, :], windows[1][:])

@@ -21,6 +21,7 @@ M_TILES = N // P
 W = 128
 CHUNKS = S // W
 RUN = 4
+QUAD = 32
 
 
 def tile_picked_place_lin_none_sub_l_kernel(tc, xT, w_words, w_scales, gate, offs, out):
@@ -36,17 +37,22 @@ def tile_picked_place_lin_none_sub_l_kernel(tc, xT, w_words, w_scales, gate, off
         offsets = keep.tile([P, S // 16], U16, name="offsets")
         w_codes = keep.tile([P, PASSES, N], U32, name="w_codes", align_bytes=64)
         w_planes = keep.tile([P, N], U8, name="w_planes", align_bytes=64)
-        spark = keep.tile([P, 1], F32, name="spark")
         sparked = keep.tile([P, 1], F32, name="sparked")
         windows = [keep.tile([P, T], F32, name=f"window{h}") for h in range(M_TILES)]
         grouped = [keep.tile([P, PASSES, W * PACK], BF16, name=f"grouped{c}", align_bytes=64) for c in range(CHUNKS)]
         codes = [keep.tile([P, PASSES, W], U32, name=f"codes{c}", align_bytes=64) for c in range(CHUNKS)]
         planes = [keep.tile([P, PASSES, W], U8, name=f"planes{c}", align_bytes=64) for c in range(CHUNKS)]
         raws = [[keep.tile([P, PACK, W], F32, name=f"raw{c}_{a}") for a in range(PASSES)] for c in range(CHUNKS)]
-        gate_first = keep.tile([P, W], F32, name="gate_first")
-        gate_rest = keep.tile([P, S - W], F32, name="gate_rest")
-        gates = [gate_first[:]] + [gate_rest[:, c * W : (c + 1) * W] for c in range(CHUNKS - 1)]
-        banks = [[psum.tile([P, W], F32, name=f"bank{c}_{h}") for h in range(M_TILES)] for c in range(CHUNKS)]
+        gate_cols = keep.tile([P, CHUNKS], F32, name="gate_cols")
+        gate_all = raws[0][0][:].rearrange("p t j -> p (t j)")
+        gates = [gate_all[:, c * W : (c + 1) * W] for c in range(CHUNKS)]
+        ones = keep.tile([P, QUAD], F32, name="ones")
+        ramp = keep.tile([P, QUAD], F32, name="ramp", align_bytes=64)
+        ramp_t = keep.tile([P, QUAD], F32, name="ramp_t", align_bytes=64)
+        identity = keep.tile([P, P], F32, name="identity")
+        full_banks = [[psum.tile([P, S], F32, name=f"bank{c}_{h}") for h in range(M_TILES)] for c in range(CHUNKS)]
+        banks = [[bank[:, 0:W] for bank in pair] for pair in full_banks]
+        gate_bank = full_banks[CHUNKS - 1][M_TILES - 1][:].rearrange("p (e n) -> p e n", e=CHUNKS)
         sums = [[keep.tile([P, W], F32, name=f"sums{c}_{h}")[:] if (c, h) not in [(0, 1), (1, 0), (1, 1), (2, 0), (2, 1)] else None for h in range(M_TILES)] for c in range(CHUNKS)]
         sums[0][1] = raws[1][1][:, 0, :]
         for c in (1, 2):
@@ -54,26 +60,34 @@ def tile_picked_place_lin_none_sub_l_kernel(tc, xT, w_words, w_scales, gate, off
                 sums[c][h] = raws[c + 1][1][:, h, :]
 
         nc.vector.memset(w_planes[:].bitcast(I32), 0)
-        nc.vector.memset(spark[:], 0.0)
-        nc.scalar.copy(sparked[:], spark[:])
+        nc.vector.memset(ones[:], 1.0)
+        nc.scalar.copy(sparked[:], ones[:, 0:1])
+        nc.vector.memset(identity[:], 0.0)
+        nc.vector.tensor_tensor_scan(ramp[:], ones[:], ones[:], 0.0, MULT, mybir.AluOpType.add)
+        nc.vector.transpose(ramp_t[:], ramp[:])
+        for q in range(P // QUAD):
+            rows = slice(q * QUAD, (q + 1) * QUAD)
+            nc.vector.tensor_tensor(identity[rows, rows], ramp[rows, :], ramp_t[rows, :], mybir.AluOpType.is_equal)
 
         def load_x(c, a):
             nc.sync.dma_start(raws[c][a][:], x_rows[a][:, :, c * W : (c + 1) * W])
 
+        nc.sync.dma_start(gate_cols[:], gate[0].rearrange("(n e) -> n e", e=CHUNKS))
         nc.sync.dma_start(offsets[:], offs)
         load_x(0, 0)
         load_x(0, 1)
         nc.sync.dma_start(w_codes[:].bitcast(I32), w_rows)
         for q in range(4):
             nc.sync.dma_start(w_planes[32 * q : 32 * q + 4 * PASSES, :].bitcast(I32), scale_rows[q])
-        nc.gpsimd.dma_start(gate_first[:], gate[0:P, 0:W])
         for c in range(1, CHUNKS):
             for a in range(PASSES):
                 load_x(c, a)
-            if c == 2:
-                nc.sync.dma_start(gate_rest[:], gate[0:P, W:S])
         for h in range(M_TILES):
-            nc.vector.memset(windows[h][:], 0.0)
+            for half in range(2):
+                nc.vector.memset(windows[h][:, half * S : (half + 1) * S], 0.0)
+
+        for e in range(CHUNKS):
+            nc.tensor.transpose(gate_bank[:, e, :], gate_cols[:, e : e + 1].to_broadcast([P, P]), identity[:])
 
         def pack(c, a):
             dst = grouped[c][:, a, :].rearrange("p (c i t) -> p c t i", i=RUN, t=PACK)
@@ -90,7 +104,7 @@ def tile_picked_place_lin_none_sub_l_kernel(tc, xT, w_words, w_scales, gate, off
             cols = slice(h * P, (h + 1) * P)
             for a in range(PASSES):
                 nc.tensor.matmul_mx(
-                    out=banks[c][h][:],
+                    out=banks[c][h],
                     lhsT=w_codes[:, a, cols].bitcast(FP8X4),
                     lhsT_scale=w_planes[4 * a : P, cols],
                     rhs=codes[c][:, a, :].bitcast(FP8X4),
@@ -101,9 +115,9 @@ def tile_picked_place_lin_none_sub_l_kernel(tc, xT, w_words, w_scales, gate, off
 
         def unload(c, h):
             if (c, h) == (0, 0):
-                nc.vector.tensor_copy(sums[c][h], banks[c][h][:])
+                nc.vector.tensor_copy(sums[c][h], banks[c][h])
             else:
-                nc.scalar.copy(sums[c][h], banks[c][h][:])
+                nc.scalar.copy(sums[c][h], banks[c][h])
 
         def scatter(c, h):
             places = offsets[:, c * (W // 16) : (c + 1) * (W // 16)]
@@ -125,6 +139,7 @@ def tile_picked_place_lin_none_sub_l_kernel(tc, xT, w_words, w_scales, gate, off
                 multiply(c, h)
 
         products(0)
+        nc.scalar.copy(gate_all.rearrange("p (n e) -> p n e", e=CHUNKS), gate_bank.rearrange("p e n -> p n e"))
         finish(0, 0)
         products(1)
         finish(0, 1)

@@ -59,7 +59,7 @@ def tile_picked_place_lin_none_sub_l_kernel(tc, xT, w_words, w_scales, gate, off
             for h in range(M_TILES):
                 sums[c][h] = raws[c + 1][1][:, h, :]
 
-        nc.vector.memset(w_planes[:].bitcast(I32), 0)
+        nc.gpsimd.memset(w_planes[:].bitcast(I32), 0)
         nc.vector.memset(ones[:], 1.0)
         nc.scalar.copy(sparked[:], ones[:, 0:1])
         nc.vector.memset(identity[:], 0.0)
@@ -72,16 +72,18 @@ def tile_picked_place_lin_none_sub_l_kernel(tc, xT, w_words, w_scales, gate, off
         def load_x(c, a):
             nc.sync.dma_start(raws[c][a][:], x_rows[a][:, :, c * W : (c + 1) * W])
 
-        nc.sync.dma_start(gate_cols[:], gate[0].rearrange("(n e) -> n e", e=CHUNKS))
-        nc.sync.dma_start(offsets[:], offs)
         load_x(0, 0)
+        nc.sync.dma_start(gate_cols[:], gate[0].rearrange("(n e) -> n e", e=CHUNKS))
         load_x(0, 1)
         nc.sync.dma_start(w_codes[:].bitcast(I32), w_rows)
         for q in range(4):
-            nc.sync.dma_start(w_planes[32 * q : 32 * q + 4 * PASSES, :].bitcast(I32), scale_rows[q])
+            queue = nc.gpsimd if q == 3 else nc.sync
+            queue.dma_start(w_planes[32 * q : 32 * q + 4 * PASSES, :].bitcast(I32), scale_rows[q])
         for c in range(1, CHUNKS):
             for a in range(PASSES):
                 load_x(c, a)
+                if (c, a) == (1, 0):
+                    nc.sync.dma_start(offsets[:], offs)
         for h in range(M_TILES):
             for half in range(2):
                 nc.vector.memset(windows[h][:, half * S : (half + 1) * S], 0.0)
@@ -92,7 +94,7 @@ def tile_picked_place_lin_none_sub_l_kernel(tc, xT, w_words, w_scales, gate, off
         def pack(c, a):
             dst = grouped[c][:, a, :].rearrange("p (c i t) -> p c t i", i=RUN, t=PACK)
             src = raws[c][a][:].rearrange("p t (c i) -> p c t i", i=RUN)
-            if (c, a) == (0, 1):
+            if (c, a) in [(0, 1), (1, 0)]:
                 nc.vector.tensor_copy(dst, src)
             else:
                 nc.scalar.copy(dst, src)
@@ -114,10 +116,7 @@ def tile_picked_place_lin_none_sub_l_kernel(tc, xT, w_words, w_scales, gate, off
                 )
 
         def unload(c, h):
-            if (c, h) == (0, 0):
-                nc.vector.tensor_copy(sums[c][h], banks[c][h])
-            else:
-                nc.scalar.copy(sums[c][h], banks[c][h])
+            nc.scalar.copy(sums[c][h], banks[c][h])
 
         def scatter(c, h):
             places = offsets[:, c * (W // 16) : (c + 1) * (W // 16)]

@@ -22,12 +22,13 @@ W = 128
 CHUNKS = S // W
 RUN = 4
 QUAD = 32
+SPLIT = 80 // RUN
 
 
 def tile_picked_place_lin_none_sub_l_kernel(tc, xT, w_words, w_scales, gate, offs, out):
     nc = tc.nc
     x_rows = xT.rearrange("(a p t) j -> a p t j", a=PASSES, t=PACK)
-    w_rows = w_words.rearrange("a p m r -> p a (m r)").bitcast(I32)
+    w_rows = w_words.rearrange("a p (h m) r -> h p a (m r)", h=M_TILES).bitcast(I32)
     scale_rows = w_scales.rearrange("a (q i) m -> q a i m", i=4).bitcast(I32)
 
     with ExitStack() as ctx:
@@ -35,7 +36,7 @@ def tile_picked_place_lin_none_sub_l_kernel(tc, xT, w_words, w_scales, gate, off
         psum = ctx.enter_context(tc.psum_pool(name="psum", bufs=1))
 
         offsets = keep.tile([P, S // 16], U16, name="offsets")
-        w_codes = keep.tile([P, PASSES, N], U32, name="w_codes", align_bytes=64)
+        w_codes = [keep.tile([P, PASSES, P], U32, name=f"w_codes{h}", align_bytes=64) for h in range(M_TILES)]
         w_planes = keep.tile([P, N], U8, name="w_planes", align_bytes=64)
         sparked = keep.tile([P, 1], F32, name="sparked")
         windows = [keep.tile([P, T], F32, name=f"window{h}") for h in range(M_TILES)]
@@ -53,11 +54,14 @@ def tile_picked_place_lin_none_sub_l_kernel(tc, xT, w_words, w_scales, gate, off
         full_banks = [[psum.tile([P, S], F32, name=f"bank{c}_{h}") for h in range(M_TILES)] for c in range(CHUNKS)]
         banks = [[bank[:, 0:W] for bank in pair] for pair in full_banks]
         gate_bank = full_banks[CHUNKS - 1][M_TILES - 1][:].rearrange("p (e n) -> p e n", e=CHUNKS)
-        sums = [[keep.tile([P, W], F32, name=f"sums{c}_{h}")[:] if (c, h) not in [(0, 1), (1, 0), (1, 1), (2, 0), (2, 1)] else None for h in range(M_TILES)] for c in range(CHUNKS)]
-        sums[0][1] = raws[1][1][:, 0, :]
-        for c in (1, 2):
-            for h in range(M_TILES):
-                sums[c][h] = raws[c + 1][1][:, h, :]
+        own_sums = [keep.tile([P, W], F32, name=f"own_sums{u}") for u in range(2)]
+        last_sums = keep.tile([P, 2 * W], F32, name="last_sums")
+        sums = [
+            [own_sums[0][:], raws[1][1][:, 0, :]],
+            [raws[2][0][:, 0, :], raws[3][0][:, 1, :]],
+            [raws[3][0][:, 0, :], last_sums[:, 0:W]],
+            [own_sums[1][:], last_sums[:, W : 2 * W]],
+        ]
 
         nc.gpsimd.memset(w_planes[:].bitcast(I32), 0)
         nc.vector.memset(ones[:], 1.0)
@@ -75,7 +79,7 @@ def tile_picked_place_lin_none_sub_l_kernel(tc, xT, w_words, w_scales, gate, off
         load_x(0, 0)
         nc.sync.dma_start(gate_cols[:], gate[0].rearrange("(n e) -> n e", e=CHUNKS))
         load_x(0, 1)
-        nc.sync.dma_start(w_codes[:].bitcast(I32), w_rows)
+        nc.sync.dma_start(w_codes[0][:].bitcast(I32), w_rows[0])
         for q in range(4):
             queue = nc.gpsimd if q == 3 else nc.sync
             queue.dma_start(w_planes[32 * q : 32 * q + 4 * PASSES, :].bitcast(I32), scale_rows[q])
@@ -84,6 +88,8 @@ def tile_picked_place_lin_none_sub_l_kernel(tc, xT, w_words, w_scales, gate, off
                 load_x(c, a)
                 if (c, a) == (1, 0):
                     nc.sync.dma_start(offsets[:], offs)
+                if (c, a) == (1, 1):
+                    nc.sync.dma_start(w_codes[1][:].bitcast(I32), w_rows[1])
         for h in range(M_TILES):
             for half in range(2):
                 nc.vector.memset(windows[h][:, half * S : (half + 1) * S], 0.0)
@@ -94,7 +100,10 @@ def tile_picked_place_lin_none_sub_l_kernel(tc, xT, w_words, w_scales, gate, off
         def pack(c, a):
             dst = grouped[c][:, a, :].rearrange("p (c i t) -> p c t i", i=RUN, t=PACK)
             src = raws[c][a][:].rearrange("p t (c i) -> p c t i", i=RUN)
-            if (c, a) in [(0, 1), (1, 0)]:
+            if (c, a) == (0, 1):
+                nc.vector.tensor_copy(dst[:, :SPLIT], src[:, :SPLIT])
+                nc.scalar.copy(dst[:, SPLIT:], src[:, SPLIT:])
+            elif (c, a) == (1, 0):
                 nc.vector.tensor_copy(dst, src)
             else:
                 nc.scalar.copy(dst, src)
@@ -107,7 +116,7 @@ def tile_picked_place_lin_none_sub_l_kernel(tc, xT, w_words, w_scales, gate, off
             for a in range(PASSES):
                 nc.tensor.matmul_mx(
                     out=banks[c][h],
-                    lhsT=w_codes[:, a, cols].bitcast(FP8X4),
+                    lhsT=w_codes[h][:, a, :].bitcast(FP8X4),
                     lhsT_scale=w_planes[4 * a : P, cols],
                     rhs=codes[c][:, a, :].bitcast(FP8X4),
                     rhs_scale=planes[c][:, a, :],
@@ -142,11 +151,16 @@ def tile_picked_place_lin_none_sub_l_kernel(tc, xT, w_words, w_scales, gate, off
         finish(0, 0)
         products(1)
         finish(0, 1)
-        for c in range(1, CHUNKS):
-            if c + 1 < CHUNKS:
-                products(c + 1)
-            finish(c, 0)
-            if c + 1 == CHUNKS:
-                nc.sync.dma_start(out[0:P, :], windows[0][:])
-            finish(c, 1)
+        products(2)
+        finish(1, 0)
+        products(3)
+        finish(2, 0)
+        finish(1, 1)
+        finish(3, 0)
+        nc.sync.dma_start(out[0:P, :], windows[0][:])
+        unload(2, 1)
+        unload(3, 1)
+        nc.vector.tensor_tensor(
+            windows[1][:].indirect(offsets[:, 2 * (W // 16) :]), last_sums[:], gate_all[:, 2 * W :], MULT
+        )
         nc.sync.dma_start(out[P : 2 * P, :], windows[1][:])

@@ -22,13 +22,14 @@ W = 128
 CHUNKS = S // W
 RUN = 4
 QUAD = 32
+HALF = W // 2
 SPLIT = 80 // RUN
 
 
 def tile_picked_place_lin_none_sub_l_kernel(tc, xT, w_words, w_scales, gate, offs, out):
     nc = tc.nc
     x_rows = xT.rearrange("(a p t) j -> a p t j", a=PASSES, t=PACK)
-    w_rows = w_words.rearrange("a p (h m) r -> h p a (m r)", h=M_TILES).bitcast(I32)
+    w_rows = w_words.rearrange("a p m r -> p a (m r)").bitcast(I32)
     scale_rows = w_scales.rearrange("a (q i) m -> q a i m", i=4).bitcast(I32)
 
     with ExitStack() as ctx:
@@ -36,16 +37,17 @@ def tile_picked_place_lin_none_sub_l_kernel(tc, xT, w_words, w_scales, gate, off
         psum = ctx.enter_context(tc.psum_pool(name="psum", bufs=1))
 
         offsets = keep.tile([P, S // 16], U16, name="offsets")
-        w_codes = [keep.tile([P, PASSES, P], U32, name=f"w_codes{h}", align_bytes=64) for h in range(M_TILES)]
+        w_codes = keep.tile([P, PASSES, N], U32, name="w_codes", align_bytes=64)
         w_planes = keep.tile([P, N], U8, name="w_planes", align_bytes=64)
         sparked = keep.tile([P, 1], F32, name="sparked")
         windows = [keep.tile([P, T], F32, name=f"window{h}") for h in range(M_TILES)]
         grouped = [keep.tile([P, PASSES, W * PACK], BF16, name=f"grouped{c}", align_bytes=64) for c in range(CHUNKS)]
         codes = [keep.tile([P, PASSES, W], U32, name=f"codes{c}", align_bytes=64) for c in range(CHUNKS)]
         planes = [keep.tile([P, PASSES, W], U8, name=f"planes{c}", align_bytes=64) for c in range(CHUNKS)]
-        raws = [[keep.tile([P, PACK, W], F32, name=f"raw{c}_{a}") for a in range(PASSES)] for c in range(CHUNKS)]
+        padded = [[keep.tile([P, PACK, (HALF if c and a else 0) + W], F32, name=f"raw{c}_{a}") for a in range(PASSES)] for c in range(CHUNKS)]
+        raws = [[padded[c][a][:, :, (HALF if c and a else 0) :] for a in range(PASSES)] for c in range(CHUNKS)]
         gate_cols = keep.tile([P, CHUNKS], F32, name="gate_cols")
-        gate_all = raws[0][0][:].rearrange("p t j -> p (t j)")
+        gate_all = raws[0][0].rearrange("p t j -> p (t j)")
         gates = [gate_all[:, c * W : (c + 1) * W] for c in range(CHUNKS)]
         ones = keep.tile([P, QUAD], F32, name="ones")
         ramp = keep.tile([P, QUAD], F32, name="ramp", align_bytes=64)
@@ -54,13 +56,13 @@ def tile_picked_place_lin_none_sub_l_kernel(tc, xT, w_words, w_scales, gate, off
         full_banks = [[psum.tile([P, S], F32, name=f"bank{c}_{h}") for h in range(M_TILES)] for c in range(CHUNKS)]
         banks = [[bank[:, 0:W] for bank in pair] for pair in full_banks]
         gate_bank = full_banks[CHUNKS - 1][M_TILES - 1][:].rearrange("p (e n) -> p e n", e=CHUNKS)
-        own_sums = [keep.tile([P, W], F32, name=f"own_sums{u}") for u in range(2)]
+        own_sums = keep.tile([P, W], F32, name="own_sums")
         last_sums = keep.tile([P, 2 * W], F32, name="last_sums")
         sums = [
-            [own_sums[0][:], raws[1][1][:, 0, :]],
-            [raws[2][0][:, 0, :], raws[3][0][:, 1, :]],
-            [raws[3][0][:, 0, :], last_sums[:, 0:W]],
-            [own_sums[1][:], last_sums[:, W : 2 * W]],
+            [raws[1][0][:, 0, :], padded[1][1][:, 0, 0:W]],
+            [padded[2][1][:, 0, 0:W], padded[3][1][:, 1, 0:W]],
+            [padded[3][1][:, 0, 0:W], last_sums[:, 0:W]],
+            [own_sums[:], last_sums[:, W : 2 * W]],
         ]
 
         nc.gpsimd.memset(w_planes[:].bitcast(I32), 0)
@@ -74,22 +76,20 @@ def tile_picked_place_lin_none_sub_l_kernel(tc, xT, w_words, w_scales, gate, off
             nc.vector.tensor_tensor(identity[rows, rows], ramp[rows, :], ramp_t[rows, :], mybir.AluOpType.is_equal)
 
         def load_x(c, a):
-            nc.sync.dma_start(raws[c][a][:], x_rows[a][:, :, c * W : (c + 1) * W])
+            nc.sync.dma_start(raws[c][a], x_rows[a][:, :, c * W : (c + 1) * W])
 
         load_x(0, 0)
         nc.sync.dma_start(gate_cols[:], gate[0].rearrange("(n e) -> n e", e=CHUNKS))
         load_x(0, 1)
-        nc.sync.dma_start(w_codes[0][:].bitcast(I32), w_rows[0])
+        nc.sync.dma_start(w_codes[:].bitcast(I32), w_rows)
         for q in range(4):
             queue = nc.gpsimd if q == 3 else nc.sync
             queue.dma_start(w_planes[32 * q : 32 * q + 4 * PASSES, :].bitcast(I32), scale_rows[q])
         for c in range(1, CHUNKS):
             for a in range(PASSES):
                 load_x(c, a)
-                if (c, a) == (1, 0):
-                    nc.sync.dma_start(offsets[:], offs)
                 if (c, a) == (1, 1):
-                    nc.sync.dma_start(w_codes[1][:].bitcast(I32), w_rows[1])
+                    nc.sync.dma_start(offsets[:], offs)
         for h in range(M_TILES):
             for half in range(2):
                 nc.vector.memset(windows[h][:, half * S : (half + 1) * S], 0.0)
@@ -99,14 +99,17 @@ def tile_picked_place_lin_none_sub_l_kernel(tc, xT, w_words, w_scales, gate, off
 
         def pack(c, a):
             dst = grouped[c][:, a, :].rearrange("p (c i t) -> p c t i", i=RUN, t=PACK)
-            src = raws[c][a][:].rearrange("p t (c i) -> p c t i", i=RUN)
+            src = raws[c][a].rearrange("p t (c i) -> p c t i", i=RUN)
             if (c, a) == (0, 1):
                 nc.vector.tensor_copy(dst[:, :SPLIT], src[:, :SPLIT])
                 nc.scalar.copy(dst[:, SPLIT:], src[:, SPLIT:])
             elif (c, a) == (1, 0):
                 nc.vector.tensor_copy(dst, src)
-            else:
+            elif a == 0:
                 nc.scalar.copy(dst, src)
+            else:
+                nc.scalar.copy(dst[:, : HALF // RUN], src[:, : HALF // RUN])
+                nc.scalar.copy(dst[:, HALF // RUN :], src[:, HALF // RUN :])
 
         def quantize(c, a):
             nc.vector.quantize_mx(out=codes[c][:, a, :].bitcast(FP8X4), scales=planes[c][:, a, :], in_=grouped[c][:, a, :])
@@ -116,7 +119,7 @@ def tile_picked_place_lin_none_sub_l_kernel(tc, xT, w_words, w_scales, gate, off
             for a in range(PASSES):
                 nc.tensor.matmul_mx(
                     out=banks[c][h],
-                    lhsT=w_codes[h][:, a, :].bitcast(FP8X4),
+                    lhsT=w_codes[:, a, cols].bitcast(FP8X4),
                     lhsT_scale=w_planes[4 * a : P, cols],
                     rhs=codes[c][:, a, :].bitcast(FP8X4),
                     rhs_scale=planes[c][:, a, :],
@@ -125,7 +128,10 @@ def tile_picked_place_lin_none_sub_l_kernel(tc, xT, w_words, w_scales, gate, off
                 )
 
         def unload(c, h):
-            nc.scalar.copy(sums[c][h], banks[c][h])
+            if (c, h) == (0, 0):
+                nc.vector.tensor_copy(sums[c][h], banks[c][h])
+            else:
+                nc.scalar.copy(sums[c][h], banks[c][h])
 
         def scatter(c, h):
             places = offsets[:, c * (W // 16) : (c + 1) * (W // 16)]
@@ -148,8 +154,13 @@ def tile_picked_place_lin_none_sub_l_kernel(tc, xT, w_words, w_scales, gate, off
 
         products(0)
         nc.scalar.copy(gate_all.rearrange("p (n e) -> p n e", e=CHUNKS), gate_bank.rearrange("p e n -> p n e"))
+        pack(1, 0)
+        quantize(1, 0)
         finish(0, 0)
-        products(1)
+        pack(1, 1)
+        quantize(1, 1)
+        for h in range(M_TILES):
+            multiply(1, h)
         finish(0, 1)
         products(2)
         finish(1, 0)

@@ -12,25 +12,29 @@ U32 = mybir.dt.uint32
 U16 = mybir.dt.uint16
 U8 = mybir.dt.uint8
 FP8X4 = mybir.dt.float8_e4m3fn_x4
-MULT = mybir.AluOpType.mult
+ALU = mybir.AluOpType
 
 P = 128
 PACK = 4
 PASSES = K // (P * PACK)
-M_TILES = N // P
+GROUPS = N // P
 W = 128
 CHUNKS = S // W
-RUN = 4
-QUAD = 32
 HALF = W // 2
-SPLIT = 80 // RUN
+LIST_COLS = W // 16
+QUAD = 32
+QUADS = P // QUAD
+SCALE_ROWS = 4
+GATE_RUN = S // P
+RUN = 4
+VECTOR_COLS = 80
 
 
 def tile_picked_place_lin_none_sub_l_kernel(tc, xT, w_words, w_scales, gate, offs, out):
     nc = tc.nc
     x_rows = xT.rearrange("(a p t) j -> a p t j", a=PASSES, t=PACK)
     w_rows = w_words.rearrange("a p m r -> p a (m r)").bitcast(I32)
-    scale_rows = w_scales.rearrange("a (q i) m -> q a i m", i=4).bitcast(I32)
+    scale_rows = w_scales.rearrange("a (q i) m -> q a i m", i=SCALE_ROWS).bitcast(I32)
 
     with ExitStack() as ctx:
         keep = ctx.enter_context(tc.tile_pool(name="keep", bufs=1))
@@ -39,23 +43,26 @@ def tile_picked_place_lin_none_sub_l_kernel(tc, xT, w_words, w_scales, gate, off
         offsets = keep.tile([P, S // 16], U16, name="offsets")
         w_codes = keep.tile([P, PASSES, N], U32, name="w_codes", align_bytes=64)
         w_planes = keep.tile([P, N], U8, name="w_planes", align_bytes=64)
-        sparked = keep.tile([P, 1], F32, name="sparked")
-        windows = [keep.tile([P, T], F32, name=f"window{h}") for h in range(M_TILES)]
+        windows = [keep.tile([P, T], F32, name=f"window{h}") for h in range(GROUPS)]
         grouped = [keep.tile([P, PASSES, W * PACK], BF16, name=f"grouped{c}", align_bytes=64) for c in range(CHUNKS)]
         codes = [keep.tile([P, PASSES, W], U32, name=f"codes{c}", align_bytes=64) for c in range(CHUNKS)]
         planes = [keep.tile([P, PASSES, W], U8, name=f"planes{c}", align_bytes=64) for c in range(CHUNKS)]
-        padded = [[keep.tile([P, PACK, (HALF if c and a else 0) + W], F32, name=f"raw{c}_{a}") for a in range(PASSES)] for c in range(CHUNKS)]
-        raws = [[padded[c][a][:, :, (HALF if c and a else 0) :] for a in range(PASSES)] for c in range(CHUNKS)]
-        gate_cols = keep.tile([P, CHUNKS], F32, name="gate_cols")
+        spare = [[HALF if c > 0 and a == PASSES - 1 else 0 for a in range(PASSES)] for c in range(CHUNKS)]
+        padded = [
+            [keep.tile([P, PACK, spare[c][a] + W], F32, name=f"raw{c}_{a}") for a in range(PASSES)]
+            for c in range(CHUNKS)
+        ]
+        raws = [[padded[c][a][:, :, spare[c][a] :] for a in range(PASSES)] for c in range(CHUNKS)]
+        gate_cols = keep.tile([P, GATE_RUN], F32, name="gate_cols")
         gate_all = raws[0][0].rearrange("p t j -> p (t j)")
-        gates = [gate_all[:, c * W : (c + 1) * W] for c in range(CHUNKS)]
         ones = keep.tile([P, QUAD], F32, name="ones")
         ramp = keep.tile([P, QUAD], F32, name="ramp", align_bytes=64)
         ramp_t = keep.tile([P, QUAD], F32, name="ramp_t", align_bytes=64)
         identity = keep.tile([P, P], F32, name="identity")
-        full_banks = [[psum.tile([P, S], F32, name=f"bank{c}_{h}") for h in range(M_TILES)] for c in range(CHUNKS)]
+        full_banks = [[psum.tile([P, S], F32, name=f"bank{c}_{h}") for h in range(GROUPS)] for c in range(CHUNKS)]
         banks = [[bank[:, 0:W] for bank in pair] for pair in full_banks]
-        gate_bank = full_banks[CHUNKS - 1][M_TILES - 1][:].rearrange("p (e n) -> p e n", e=CHUNKS)
+        gate_bank = full_banks[CHUNKS - 1][GROUPS - 1][:].rearrange("p (e n) -> p e n", e=GATE_RUN)
+
         own_sums = keep.tile([P, W], F32, name="own_sums")
         last_sums = keep.tile([P, 2 * W], F32, name="last_sums")
         sums = [
@@ -66,101 +73,108 @@ def tile_picked_place_lin_none_sub_l_kernel(tc, xT, w_words, w_scales, gate, off
         ]
 
         nc.gpsimd.memset(w_planes[:].bitcast(I32), 0)
+
         nc.vector.memset(ones[:], 1.0)
-        nc.scalar.copy(sparked[:], ones[:, 0:1])
         nc.vector.memset(identity[:], 0.0)
-        nc.vector.tensor_tensor_scan(ramp[:], ones[:], ones[:], 0.0, MULT, mybir.AluOpType.add)
+        nc.vector.tensor_tensor_scan(ramp[:], ones[:], ones[:], 0.0, ALU.mult, ALU.add)
         nc.vector.transpose(ramp_t[:], ramp[:])
-        for q in range(P // QUAD):
+        for q in range(QUADS):
             rows = slice(q * QUAD, (q + 1) * QUAD)
-            nc.vector.tensor_tensor(identity[rows, rows], ramp[rows, :], ramp_t[rows, :], mybir.AluOpType.is_equal)
+            nc.vector.tensor_tensor(identity[rows, rows], ramp[rows, :], ramp_t[rows, :], ALU.is_equal)
 
         def load_x(c, a):
             nc.sync.dma_start(raws[c][a], x_rows[a][:, :, c * W : (c + 1) * W])
 
         load_x(0, 0)
-        nc.sync.dma_start(gate_cols[:], gate[0].rearrange("(n e) -> n e", e=CHUNKS))
+        nc.sync.dma_start(gate_cols[:], gate[0].rearrange("(n e) -> n e", e=GATE_RUN))
         load_x(0, 1)
         nc.sync.dma_start(w_codes[:].bitcast(I32), w_rows)
-        for q in range(4):
-            queue = nc.gpsimd if q == 3 else nc.sync
-            queue.dma_start(w_planes[32 * q : 32 * q + 4 * PASSES, :].bitcast(I32), scale_rows[q])
-        for c in range(1, CHUNKS):
+        for q in range(QUADS):
+            queue = nc.gpsimd if q == QUADS - 1 else nc.sync
+            queue.dma_start(w_planes[QUAD * q : QUAD * q + SCALE_ROWS * PASSES, :].bitcast(I32), scale_rows[q])
+        for a in range(PASSES):
+            load_x(1, a)
+        nc.sync.dma_start(offsets[:], offs)
+        for c in range(2, CHUNKS):
             for a in range(PASSES):
                 load_x(c, a)
-                if (c, a) == (1, 1):
-                    nc.sync.dma_start(offsets[:], offs)
-        for h in range(M_TILES):
-            for half in range(2):
-                nc.vector.memset(windows[h][:, half * S : (half + 1) * S], 0.0)
 
-        for e in range(CHUNKS):
+        halves = [windows[h][:, u * S : (u + 1) * S] for h in range(GROUPS) for u in range(T // S)]
+        for half in halves[:-1]:
+            nc.vector.memset(half, 0.0)
+        nc.scalar.copy(halves[-1], halves[0])
+
+        for e in range(GATE_RUN):
             nc.tensor.transpose(gate_bank[:, e, :], gate_cols[:, e : e + 1].to_broadcast([P, P]), identity[:])
 
+        def pack_columns(copy, c, a, lo, hi):
+            dst = grouped[c][:, a, :].rearrange("p (b i t) -> p b t i", i=RUN, t=PACK)
+            src = raws[c][a].rearrange("p t (b i) -> p b t i", i=RUN)
+            copy(dst[:, lo // RUN : hi // RUN], src[:, lo // RUN : hi // RUN])
+
         def pack(c, a):
-            dst = grouped[c][:, a, :].rearrange("p (c i t) -> p c t i", i=RUN, t=PACK)
-            src = raws[c][a].rearrange("p t (c i) -> p c t i", i=RUN)
             if (c, a) == (0, 1):
-                nc.vector.tensor_copy(dst[:, :SPLIT], src[:, :SPLIT])
-                nc.scalar.copy(dst[:, SPLIT:], src[:, SPLIT:])
+                pack_columns(nc.vector.tensor_copy, c, a, 0, VECTOR_COLS)
+                pack_columns(nc.scalar.copy, c, a, VECTOR_COLS, W)
             elif (c, a) == (1, 0):
-                nc.vector.tensor_copy(dst, src)
+                pack_columns(nc.vector.tensor_copy, c, a, 0, W)
             elif a == 0:
-                nc.scalar.copy(dst, src)
+                pack_columns(nc.scalar.copy, c, a, 0, W)
             else:
-                nc.scalar.copy(dst[:, : HALF // RUN], src[:, : HALF // RUN])
-                nc.scalar.copy(dst[:, HALF // RUN :], src[:, HALF // RUN :])
+                pack_columns(nc.scalar.copy, c, a, 0, HALF)
+                pack_columns(nc.scalar.copy, c, a, HALF, W)
 
         def quantize(c, a):
-            nc.vector.quantize_mx(out=codes[c][:, a, :].bitcast(FP8X4), scales=planes[c][:, a, :], in_=grouped[c][:, a, :])
+            nc.vector.quantize_mx(
+                out=codes[c][:, a, :].bitcast(FP8X4), scales=planes[c][:, a, :], in_=grouped[c][:, a, :]
+            )
 
-        def multiply(c, h):
-            cols = slice(h * P, (h + 1) * P)
-            for a in range(PASSES):
-                nc.tensor.matmul_mx(
-                    out=banks[c][h],
-                    lhsT=w_codes[:, a, cols].bitcast(FP8X4),
-                    lhsT_scale=w_planes[4 * a : P, cols],
-                    rhs=codes[c][:, a, :].bitcast(FP8X4),
-                    rhs_scale=planes[c][:, a, :],
-                    start=(a == 0),
-                    stop=(a == PASSES - 1),
-                )
+        def multiply(c):
+            for h in range(GROUPS):
+                cols = slice(h * P, (h + 1) * P)
+                for a in range(PASSES):
+                    nc.tensor.matmul_mx(
+                        out=banks[c][h],
+                        lhsT=w_codes[:, a, cols].bitcast(FP8X4),
+                        lhsT_scale=w_planes[SCALE_ROWS * a : P, cols],
+                        rhs=codes[c][:, a, :].bitcast(FP8X4),
+                        rhs_scale=planes[c][:, a, :],
+                        start=(a == 0),
+                        stop=(a == PASSES - 1),
+                    )
 
-        def unload(c, h):
-            if (c, h) == (0, 0):
-                nc.vector.tensor_copy(sums[c][h], banks[c][h])
-            else:
-                nc.scalar.copy(sums[c][h], banks[c][h])
-
-        def scatter(c, h):
-            places = offsets[:, c * (W // 16) : (c + 1) * (W // 16)]
-            nc.vector.tensor_tensor(windows[h][:].indirect(places), sums[c][h], gates[c], MULT)
-
-        def prepare(c):
+        def products(c):
             for a in range(PASSES):
                 pack(c, a)
             for a in range(PASSES):
                 quantize(c, a)
+            multiply(c)
+
+        def unload(c, h):
+            copy = nc.vector.tensor_copy if (c, h) == (0, 0) else nc.scalar.copy
+            copy(sums[c][h], banks[c][h])
+
+        def scatter(h, values, first, last):
+            places = offsets[:, first * LIST_COLS : (last + 1) * LIST_COLS]
+            nc.vector.tensor_tensor(
+                windows[h][:].indirect(places), values, gate_all[:, first * W : (last + 1) * W], ALU.mult
+            )
 
         def finish(c, h):
             unload(c, h)
-            scatter(c, h)
+            scatter(h, sums[c][h], c, c)
 
-        def products(c):
-            prepare(c)
-            for h in range(M_TILES):
-                multiply(c, h)
+        def store(h):
+            nc.sync.dma_start(out[h * P : (h + 1) * P, :], windows[h][:])
 
         products(0)
-        nc.scalar.copy(gate_all.rearrange("p (n e) -> p n e", e=CHUNKS), gate_bank.rearrange("p e n -> p n e"))
+        nc.scalar.copy(gate_all.rearrange("p (n e) -> p n e", e=GATE_RUN), gate_bank.rearrange("p e n -> p n e"))
         pack(1, 0)
         quantize(1, 0)
         finish(0, 0)
         pack(1, 1)
         quantize(1, 1)
-        for h in range(M_TILES):
-            multiply(1, h)
+        multiply(1)
         finish(0, 1)
         products(2)
         finish(1, 0)
@@ -168,10 +182,8 @@ def tile_picked_place_lin_none_sub_l_kernel(tc, xT, w_words, w_scales, gate, off
         finish(2, 0)
         finish(1, 1)
         finish(3, 0)
-        nc.sync.dma_start(out[0:P, :], windows[0][:])
+        store(0)
         unload(2, 1)
         unload(3, 1)
-        nc.vector.tensor_tensor(
-            windows[1][:].indirect(offsets[:, 2 * (W // 16) :]), last_sums[:], gate_all[:, 2 * W :], MULT
-        )
-        nc.sync.dma_start(out[P : 2 * P, :], windows[1][:])
+        scatter(1, last_sums[:], 2, 3)
+        store(1)

@@ -27,7 +27,7 @@ QUADS = P // QUAD
 SCALE_ROWS = 4
 GATE_RUN = S // P
 RUN = 4
-VECTOR_COLS = 80
+VECTOR_COLS = (80, 48)
 
 
 def tile_picked_place_lin_none_sub_l_kernel(tc, xT, w_words, w_scales, gate, offs, out):
@@ -41,20 +41,22 @@ def tile_picked_place_lin_none_sub_l_kernel(tc, xT, w_words, w_scales, gate, off
         psum = ctx.enter_context(tc.psum_pool(name="psum", bufs=1))
 
         offsets = keep.tile([P, S // 16], U16, name="offsets")
-        w_codes = keep.tile([P, PASSES, N], U32, name="w_codes", align_bytes=64)
+        w_codes = [keep.tile([P, PASSES, P], U32, name=f"w_codes{h}", align_bytes=64) for h in range(GROUPS)]
         w_planes = keep.tile([P, N], U8, name="w_planes", align_bytes=64)
         windows = [keep.tile([P, T], F32, name=f"window{h}") for h in range(GROUPS)]
         grouped = [keep.tile([P, PASSES, W * PACK], BF16, name=f"grouped{c}", align_bytes=64) for c in range(CHUNKS)]
         codes = [keep.tile([P, PASSES, W], U32, name=f"codes{c}", align_bytes=64) for c in range(CHUNKS)]
         planes = [keep.tile([P, PASSES, W], U8, name=f"planes{c}", align_bytes=64) for c in range(CHUNKS)]
-        spare = [[HALF if c > 0 and a == PASSES - 1 else 0 for a in range(PASSES)] for c in range(CHUNKS)]
-        padded = [
-            [keep.tile([P, PACK, spare[c][a] + W], F32, name=f"raw{c}_{a}") for a in range(PASSES)]
-            for c in range(CHUNKS)
-        ]
-        raws = [[padded[c][a][:, :, spare[c][a] :] for a in range(PASSES)] for c in range(CHUNKS)]
+        wide = [keep.tile([P, PACK, 2 * W], F32, name=f"wide{a}") for a in range(PASSES)]
+        spare = {2: [HALF, HALF], 3: [0, HALF]}
+        padded = {
+            c: [keep.tile([P, PACK, spare[c][a] + W], F32, name=f"raw{c}_{a}") for a in range(PASSES)]
+            for c in range(2, CHUNKS)
+        }
+        raws = [[wide[a][:, :, c * W : (c + 1) * W] for a in range(PASSES)] for c in range(2)]
+        raws = raws + [[padded[c][a][:, :, spare[c][a] :] for a in range(PASSES)] for c in range(2, CHUNKS)]
         gate_cols = keep.tile([P, GATE_RUN], F32, name="gate_cols")
-        gate_all = raws[0][0].rearrange("p t j -> p (t j)")
+        gate_all = wide[1][:, 0:2, :].rearrange("p t j -> p (t j)")
         ones = keep.tile([P, QUAD], F32, name="ones")
         ramp = keep.tile([P, QUAD], F32, name="ramp", align_bytes=64)
         ramp_t = keep.tile([P, QUAD], F32, name="ramp_t", align_bytes=64)
@@ -63,10 +65,11 @@ def tile_picked_place_lin_none_sub_l_kernel(tc, xT, w_words, w_scales, gate, off
         banks = [[bank[:, 0:W] for bank in pair] for pair in full_banks]
         gate_bank = full_banks[CHUNKS - 1][GROUPS - 1][:].rearrange("p (e n) -> p e n", e=GATE_RUN)
 
+        first_sums = [keep.tile([P, W], F32, name=f"first_sums{h}") for h in range(GROUPS)]
         own_sums = keep.tile([P, W], F32, name="own_sums")
         last_sums = keep.tile([P, 2 * W], F32, name="last_sums")
         sums = [
-            [raws[1][0][:, 0, :], padded[1][1][:, 0, 0:W]],
+            [first_sums[0][:], padded[2][0][:, 0, 0:W]],
             [padded[2][1][:, 0, 0:W], padded[3][1][:, 1, 0:W]],
             [padded[3][1][:, 0, 0:W], last_sums[:, 0:W]],
             [own_sums[:], last_sums[:, W : 2 * W]],
@@ -82,19 +85,25 @@ def tile_picked_place_lin_none_sub_l_kernel(tc, xT, w_words, w_scales, gate, off
             rows = slice(q * QUAD, (q + 1) * QUAD)
             nc.vector.tensor_tensor(identity[rows, rows], ramp[rows, :], ramp_t[rows, :], ALU.is_equal)
 
+        def load_w(h):
+            nc.sync.dma_start(w_codes[h][:].bitcast(I32), w_rows[:, :, h * P : (h + 1) * P])
+
+        def load_scales(queue, q):
+            queue.dma_start(w_planes[QUAD * q : QUAD * q + SCALE_ROWS * PASSES, :].bitcast(I32), scale_rows[q])
+
         def load_x(c, a):
             nc.sync.dma_start(raws[c][a], x_rows[a][:, :, c * W : (c + 1) * W])
 
-        load_x(0, 0)
+        nc.sync.dma_start(wide[0][:], x_rows[0][:, :, 0 : 2 * W])
         nc.sync.dma_start(gate_cols[:], gate[0].rearrange("(n e) -> n e", e=GATE_RUN))
-        load_x(0, 1)
-        nc.sync.dma_start(w_codes[:].bitcast(I32), w_rows)
-        for q in range(QUADS):
-            queue = nc.gpsimd if q == QUADS - 1 else nc.sync
-            queue.dma_start(w_planes[QUAD * q : QUAD * q + SCALE_ROWS * PASSES, :].bitcast(I32), scale_rows[q])
-        for a in range(PASSES):
-            load_x(1, a)
+        load_scales(nc.sync, 0)
+        nc.sync.dma_start(wide[1][:], x_rows[1][:, :, 0 : 2 * W])
+        load_w(0)
+        load_scales(nc.sync, 1)
+        load_scales(nc.sync, 2)
+        load_scales(nc.gpsimd, 3)
         nc.sync.dma_start(offsets[:], offs)
+        load_w(1)
         for c in range(2, CHUNKS):
             for a in range(PASSES):
                 load_x(c, a)
@@ -113,12 +122,12 @@ def tile_picked_place_lin_none_sub_l_kernel(tc, xT, w_words, w_scales, gate, off
             copy(dst[:, lo // RUN : hi // RUN], src[:, lo // RUN : hi // RUN])
 
         def pack(c, a):
-            if (c, a) == (0, 1):
-                pack_columns(nc.vector.tensor_copy, c, a, 0, VECTOR_COLS)
-                pack_columns(nc.scalar.copy, c, a, VECTOR_COLS, W)
-            elif (c, a) == (1, 0):
+            if (c, a) == (0, 0):
                 pack_columns(nc.vector.tensor_copy, c, a, 0, W)
-            elif a == 0:
+            elif c < 2 and a == 1:
+                pack_columns(nc.vector.tensor_copy, c, a, 0, VECTOR_COLS[c])
+                pack_columns(nc.scalar.copy, c, a, VECTOR_COLS[c], W)
+            elif c < 2 or spare[c][a] == 0:
                 pack_columns(nc.scalar.copy, c, a, 0, W)
             else:
                 pack_columns(nc.scalar.copy, c, a, 0, HALF)
@@ -135,7 +144,7 @@ def tile_picked_place_lin_none_sub_l_kernel(tc, xT, w_words, w_scales, gate, off
                 for a in range(PASSES):
                     nc.tensor.matmul_mx(
                         out=banks[c][h],
-                        lhsT=w_codes[:, a, cols].bitcast(FP8X4),
+                        lhsT=w_codes[h][:, a, :].bitcast(FP8X4),
                         lhsT_scale=w_planes[SCALE_ROWS * a : P, cols],
                         rhs=codes[c][:, a, :].bitcast(FP8X4),
                         rhs_scale=planes[c][:, a, :],
@@ -167,16 +176,24 @@ def tile_picked_place_lin_none_sub_l_kernel(tc, xT, w_words, w_scales, gate, off
         def store(h):
             nc.sync.dma_start(out[h * P : (h + 1) * P, :], windows[h][:])
 
-        products(0)
-        nc.scalar.copy(gate_all.rearrange("p (n e) -> p n e", e=GATE_RUN), gate_bank.rearrange("p e n -> p n e"))
+        pack(0, 0)
         pack(1, 0)
+        quantize(0, 0)
         quantize(1, 0)
-        finish(0, 0)
+        pack(0, 1)
         pack(1, 1)
+        nc.scalar.copy(gate_all.rearrange("p (n e) -> p n e", e=GATE_RUN), gate_bank.rearrange("p e n -> p n e"))
+        quantize(0, 1)
         quantize(1, 1)
+        multiply(0)
         multiply(1)
+        finish(0, 0)
+        pack(2, 0)
+        quantize(2, 0)
         finish(0, 1)
-        products(2)
+        pack(2, 1)
+        quantize(2, 1)
+        multiply(2)
         finish(1, 0)
         products(3)
         finish(2, 0)

@@ -13,6 +13,7 @@ U16 = mybir.dt.uint16
 U8 = mybir.dt.uint8
 FP8X4 = mybir.dt.float8_e4m3fn_x4
 ALU = mybir.AluOpType
+COPY = mybir.ActivationFunctionType.Copy
 
 P = 128
 PACK = 4
@@ -20,14 +21,12 @@ PASSES = K // (P * PACK)
 GROUPS = N // P
 W = 128
 CHUNKS = S // W
-HALF = W // 2
 LIST_COLS = W // 16
 QUAD = 32
 QUADS = P // QUAD
 SCALE_ROWS = 4
 GATE_RUN = S // P
 RUN = 4
-VECTOR_COLS = (80, 48)
 
 
 def tile_picked_place_lin_none_sub_l_kernel(tc, xT, w_words, w_scales, gate, offs, out):
@@ -40,23 +39,23 @@ def tile_picked_place_lin_none_sub_l_kernel(tc, xT, w_words, w_scales, gate, off
         keep = ctx.enter_context(tc.tile_pool(name="keep", bufs=1))
         psum = ctx.enter_context(tc.psum_pool(name="psum", bufs=1))
 
+        def tiles(name, shape, dtype):
+            return [
+                [keep.tile(shape, dtype, name=f"{name}{c}_{a}", align_bytes=64) for a in range(PASSES)]
+                for c in range(CHUNKS)
+            ]
+
         offsets = keep.tile([P, S // 16], U16, name="offsets")
-        w_codes = [keep.tile([P, PASSES, P], U32, name=f"w_codes{h}", align_bytes=64) for h in range(GROUPS)]
+        w_codes = keep.tile([P, PASSES, N], U32, name="w_codes", align_bytes=64)
         w_planes = keep.tile([P, N], U8, name="w_planes", align_bytes=64)
         windows = [keep.tile([P, T], F32, name=f"window{h}") for h in range(GROUPS)]
-        grouped = [keep.tile([P, PASSES, W * PACK], BF16, name=f"grouped{c}", align_bytes=64) for c in range(CHUNKS)]
-        codes = [keep.tile([P, PASSES, W], U32, name=f"codes{c}", align_bytes=64) for c in range(CHUNKS)]
-        planes = [keep.tile([P, PASSES, W], U8, name=f"planes{c}", align_bytes=64) for c in range(CHUNKS)]
-        wide = [keep.tile([P, PACK, 2 * W], F32, name=f"wide{a}") for a in range(PASSES)]
-        spare = {2: [HALF, HALF], 3: [0, HALF]}
-        padded = {
-            c: [keep.tile([P, PACK, spare[c][a] + W], F32, name=f"raw{c}_{a}") for a in range(PASSES)]
-            for c in range(2, CHUNKS)
-        }
-        raws = [[wide[a][:, :, c * W : (c + 1) * W] for a in range(PASSES)] for c in range(2)]
-        raws = raws + [[padded[c][a][:, :, spare[c][a] :] for a in range(PASSES)] for c in range(2, CHUNKS)]
+        raws = tiles("raw", [P, PACK, W], F32)
+        grouped = tiles("grouped", [P, W * PACK], BF16)
+        codes = tiles("codes", [P, W], U32)
+        planes = tiles("planes", [P, W], U8)
+        sums = tiles("sums", [P, W], F32)
         gate_cols = keep.tile([P, GATE_RUN], F32, name="gate_cols")
-        gate_all = wide[1][:, 0:2, :].rearrange("p t j -> p (t j)")
+        gate_all = keep.tile([P, S], F32, name="gate_all")
         ones = keep.tile([P, QUAD], F32, name="ones")
         ramp = keep.tile([P, QUAD], F32, name="ramp", align_bytes=64)
         ramp_t = keep.tile([P, QUAD], F32, name="ramp_t", align_bytes=64)
@@ -64,16 +63,6 @@ def tile_picked_place_lin_none_sub_l_kernel(tc, xT, w_words, w_scales, gate, off
         full_banks = [[psum.tile([P, S], F32, name=f"bank{c}_{h}") for h in range(GROUPS)] for c in range(CHUNKS)]
         banks = [[bank[:, 0:W] for bank in pair] for pair in full_banks]
         gate_bank = full_banks[CHUNKS - 1][GROUPS - 1][:].rearrange("p (e n) -> p e n", e=GATE_RUN)
-
-        first_sums = [keep.tile([P, W], F32, name=f"first_sums{h}") for h in range(GROUPS)]
-        own_sums = keep.tile([P, W], F32, name="own_sums")
-        last_sums = keep.tile([P, 2 * W], F32, name="last_sums")
-        sums = [
-            [first_sums[0][:], padded[2][0][:, 0, 0:W]],
-            [padded[2][1][:, 0, 0:W], padded[3][1][:, 1, 0:W]],
-            [padded[3][1][:, 0, 0:W], last_sums[:, 0:W]],
-            [own_sums[:], last_sums[:, W : 2 * W]],
-        ]
 
         nc.gpsimd.memset(w_planes[:].bitcast(I32), 0)
 
@@ -85,25 +74,29 @@ def tile_picked_place_lin_none_sub_l_kernel(tc, xT, w_words, w_scales, gate, off
             rows = slice(q * QUAD, (q + 1) * QUAD)
             nc.vector.tensor_tensor(identity[rows, rows], ramp[rows, :], ramp_t[rows, :], ALU.is_equal)
 
-        def load_w(h):
-            nc.sync.dma_start(w_codes[h][:].bitcast(I32), w_rows[:, :, h * P : (h + 1) * P])
+        def load_gate(queue):
+            queue.dma_start(gate_cols[:], gate[0].rearrange("(n e) -> n e", e=GATE_RUN))
+
+        def load_w():
+            nc.sync.dma_start(w_codes[:].bitcast(I32), w_rows)
 
         def load_scales(queue, q):
             queue.dma_start(w_planes[QUAD * q : QUAD * q + SCALE_ROWS * PASSES, :].bitcast(I32), scale_rows[q])
 
         def load_x(c, a):
-            nc.sync.dma_start(raws[c][a], x_rows[a][:, :, c * W : (c + 1) * W])
+            nc.sync.dma_start(raws[c][a][:], x_rows[a][:, :, c * W : (c + 1) * W])
 
-        nc.sync.dma_start(wide[0][:], x_rows[0][:, :, 0 : 2 * W])
-        nc.sync.dma_start(gate_cols[:], gate[0].rearrange("(n e) -> n e", e=GATE_RUN))
+        load_gate(nc.sync)
+        load_x(0, 0)
         load_scales(nc.sync, 0)
-        nc.sync.dma_start(wide[1][:], x_rows[1][:, :, 0 : 2 * W])
-        load_w(0)
         load_scales(nc.sync, 1)
+        load_x(0, 1)
         load_scales(nc.sync, 2)
-        load_scales(nc.gpsimd, 3)
+        load_scales(nc.sync, 3)
+        load_w()
+        load_x(1, 0)
         nc.sync.dma_start(offsets[:], offs)
-        load_w(1)
+        load_x(1, 1)
         for c in range(2, CHUNKS):
             for a in range(PASSES):
                 load_x(c, a)
@@ -111,96 +104,58 @@ def tile_picked_place_lin_none_sub_l_kernel(tc, xT, w_words, w_scales, gate, off
         halves = [windows[h][:, u * S : (u + 1) * S] for h in range(GROUPS) for u in range(T // S)]
         for half in halves[:-1]:
             nc.vector.memset(half, 0.0)
-        nc.scalar.copy(halves[-1], halves[0])
+        nc.scalar.activation(halves[-1], halves[0], COPY)
 
         for e in range(GATE_RUN):
             nc.tensor.transpose(gate_bank[:, e, :], gate_cols[:, e : e + 1].to_broadcast([P, P]), identity[:])
+        nc.scalar.copy(gate_all[:].rearrange("p (n e) -> p n e", e=GATE_RUN), gate_bank.rearrange("p e n -> p n e"))
 
-        def pack_columns(copy, c, a, lo, hi):
-            dst = grouped[c][:, a, :].rearrange("p (b i t) -> p b t i", i=RUN, t=PACK)
-            src = raws[c][a].rearrange("p t (b i) -> p b t i", i=RUN)
+        def pack(copy, c, a, lo=0, hi=W):
+            dst = grouped[c][a][:].rearrange("p (b i t) -> p b t i", i=RUN, t=PACK)
+            src = raws[c][a][:].rearrange("p t (b i) -> p b t i", i=RUN)
             copy(dst[:, lo // RUN : hi // RUN], src[:, lo // RUN : hi // RUN])
 
-        def pack(c, a):
-            if (c, a) == (0, 0):
-                pack_columns(nc.vector.tensor_copy, c, a, 0, W)
-            elif c < 2 and a == 1:
-                pack_columns(nc.vector.tensor_copy, c, a, 0, VECTOR_COLS[c])
-                pack_columns(nc.scalar.copy, c, a, VECTOR_COLS[c], W)
-            elif c < 2 or spare[c][a] == 0:
-                pack_columns(nc.scalar.copy, c, a, 0, W)
-            else:
-                pack_columns(nc.scalar.copy, c, a, 0, HALF)
-                pack_columns(nc.scalar.copy, c, a, HALF, W)
-
         def quantize(c, a):
-            nc.vector.quantize_mx(
-                out=codes[c][:, a, :].bitcast(FP8X4), scales=planes[c][:, a, :], in_=grouped[c][:, a, :]
-            )
+            nc.vector.quantize_mx(out=codes[c][a][:].bitcast(FP8X4), scales=planes[c][a][:], in_=grouped[c][a][:])
 
-        def multiply(c):
+        def multiply(c, a):
             for h in range(GROUPS):
                 cols = slice(h * P, (h + 1) * P)
-                for a in range(PASSES):
-                    nc.tensor.matmul_mx(
-                        out=banks[c][h],
-                        lhsT=w_codes[h][:, a, :].bitcast(FP8X4),
-                        lhsT_scale=w_planes[SCALE_ROWS * a : P, cols],
-                        rhs=codes[c][:, a, :].bitcast(FP8X4),
-                        rhs_scale=planes[c][:, a, :],
-                        start=(a == 0),
-                        stop=(a == PASSES - 1),
-                    )
+                nc.tensor.matmul_mx(
+                    out=banks[c][h],
+                    lhsT=w_codes[:, a, cols].bitcast(FP8X4),
+                    lhsT_scale=w_planes[SCALE_ROWS * a : P, cols],
+                    rhs=codes[c][a][:].bitcast(FP8X4),
+                    rhs_scale=planes[c][a][:],
+                    start=(a == 0),
+                    stop=(a == PASSES - 1),
+                )
 
-        def products(c):
-            for a in range(PASSES):
-                pack(c, a)
-            for a in range(PASSES):
-                quantize(c, a)
-            multiply(c)
+        def weigh(c, h):
+            nc.vector.tensor_tensor(sums[c][h][:], banks[c][h], gate_all[:, c * W : (c + 1) * W], ALU.mult)
 
-        def unload(c, h):
-            copy = nc.vector.tensor_copy if (c, h) == (0, 0) else nc.scalar.copy
-            copy(sums[c][h], banks[c][h])
+        def target(c, h):
+            return windows[h][:].indirect(offsets[:, c * LIST_COLS : (c + 1) * LIST_COLS])
 
-        def scatter(h, values, first, last):
-            places = offsets[:, first * LIST_COLS : (last + 1) * LIST_COLS]
-            nc.vector.tensor_tensor(
-                windows[h][:].indirect(places), values, gate_all[:, first * W : (last + 1) * W], ALU.mult
-            )
+        def scatter_scalar(c, h):
+            nc.scalar.activation(target(c, h), sums[c][h][:], COPY)
 
-        def finish(c, h):
-            unload(c, h)
-            scatter(h, sums[c][h], c, c)
+        def scatter_vector(c, h):
+            nc.vector.tensor_copy(target(c, h), sums[c][h][:])
 
         def store(h):
             nc.sync.dma_start(out[h * P : (h + 1) * P, :], windows[h][:])
 
-        pack(0, 0)
-        pack(1, 0)
-        quantize(0, 0)
-        quantize(1, 0)
-        pack(0, 1)
-        pack(1, 1)
-        nc.scalar.copy(gate_all.rearrange("p (n e) -> p n e", e=GATE_RUN), gate_bank.rearrange("p e n -> p n e"))
-        quantize(0, 1)
-        quantize(1, 1)
-        multiply(0)
-        multiply(1)
-        finish(0, 0)
-        pack(2, 0)
-        quantize(2, 0)
-        finish(0, 1)
-        pack(2, 1)
-        quantize(2, 1)
-        multiply(2)
-        finish(1, 0)
-        products(3)
-        finish(2, 0)
-        finish(1, 1)
-        finish(3, 0)
-        store(0)
-        unload(2, 1)
-        unload(3, 1)
-        scatter(1, last_sums[:], 2, 3)
-        store(1)
+        for c in range(CHUNKS):
+            for a in range(PASSES):
+                pack(nc.scalar.copy if (c, a) == (1, 0) else nc.vector.tensor_copy, c, a)
+                quantize(c, a)
+                multiply(c, a)
+            for h in range(GROUPS):
+                weigh(c, h)
+                if c >= 2 and h == 0:
+                    scatter_vector(c, h)
+                else:
+                    scatter_scalar(c, h)
+        for h in range(GROUPS):
+            store(h)

@@ -27,6 +27,9 @@ QUADS = P // QUAD
 SCALE_ROWS = 4
 GATE_RUN = S // P
 RUN = 4
+HALF = W // 2
+ORDER = (0, 1, 2, 3)
+VECTOR_COLS = (80, 48)
 
 
 def tile_picked_place_lin_none_sub_l_kernel(tc, xT, w_words, w_scales, gate, offs, out):
@@ -39,30 +42,42 @@ def tile_picked_place_lin_none_sub_l_kernel(tc, xT, w_words, w_scales, gate, off
         keep = ctx.enter_context(tc.tile_pool(name="keep", bufs=1))
         psum = ctx.enter_context(tc.psum_pool(name="psum", bufs=1))
 
-        def tiles(name, shape, dtype):
-            return [
-                [keep.tile(shape, dtype, name=f"{name}{c}_{a}", align_bytes=64) for a in range(PASSES)]
-                for c in range(CHUNKS)
-            ]
-
         offsets = keep.tile([P, S // 16], U16, name="offsets")
         w_codes = keep.tile([P, PASSES, N], U32, name="w_codes", align_bytes=64)
         w_planes = keep.tile([P, N], U8, name="w_planes", align_bytes=64)
         windows = [keep.tile([P, T], F32, name=f"window{h}") for h in range(GROUPS)]
-        raws = tiles("raw", [P, PACK, W], F32)
-        grouped = tiles("grouped", [P, W * PACK], BF16)
-        codes = tiles("codes", [P, W], U32)
-        planes = tiles("planes", [P, W], U8)
-        sums = tiles("sums", [P, W], F32)
+        grouped = [keep.tile([P, PASSES, W * PACK], BF16, name=f"grouped{s}", align_bytes=64) for s in range(CHUNKS)]
+        codes = [keep.tile([P, PASSES, W], U32, name=f"codes{s}", align_bytes=64) for s in range(CHUNKS)]
+        planes = [keep.tile([P, PASSES, W], U8, name=f"planes{s}", align_bytes=64) for s in range(CHUNKS)]
+        wide = [keep.tile([P, PACK, 2 * W], F32, name=f"wide{a}") for a in range(PASSES)]
+        plain = {s: keep.tile([P, PACK, W], F32, name=f"plain{s}") for s in (2, 3)}
+        padded = {s: keep.tile([P, PACK, HALF + W], F32, name=f"padded{s}") for s in (2, 3)}
+        raws = [[wide[a][:, :, s * W : (s + 1) * W] for a in range(PASSES)] for s in range(2)]
+        raws = raws + [[plain[s][:], padded[s][:, :, HALF:]] for s in (2, 3)]
         gate_cols = keep.tile([P, GATE_RUN], F32, name="gate_cols")
         gate_all = keep.tile([P, S], F32, name="gate_all")
         ones = keep.tile([P, QUAD], F32, name="ones")
         ramp = keep.tile([P, QUAD], F32, name="ramp", align_bytes=64)
         ramp_t = keep.tile([P, QUAD], F32, name="ramp_t", align_bytes=64)
         identity = keep.tile([P, P], F32, name="identity")
-        full_banks = [[psum.tile([P, S], F32, name=f"bank{c}_{h}") for h in range(GROUPS)] for c in range(CHUNKS)]
-        banks = [[bank[:, 0:W] for bank in pair] for pair in full_banks]
+        full_banks = [[psum.tile([P, S], F32, name=f"bank{s}_{h}") for h in range(GROUPS)] for s in range(CHUNKS)]
         gate_bank = full_banks[CHUNKS - 1][GROUPS - 1][:].rearrange("p (e n) -> p e n", e=GATE_RUN)
+        joint = (1,)
+        banks = [
+            [full_banks[s][0][:, h * W : (h + 1) * W] if s in joint else full_banks[s][h][:, 0:W] for h in range(GROUPS)]
+            for s in range(CHUNKS)
+        ]
+        first = keep.tile([P, GROUPS, W], F32, name="first")
+        last0 = keep.tile([P, W], F32, name="last0")
+        last1 = keep.tile([P, 2 * W], F32, name="last1")
+        weighed = [
+            [first[:, 0, :], first[:, 1, :]],
+            [padded[2][:, 0, 0:W], padded[2][:, 1, 0:W]],
+            [padded[3][:, 0, 0:W], last1[:, 0:W]],
+            [last0[:], last1[:, W : 2 * W]],
+        ]
+        banks[2][1] = full_banks[2][1][:, 0:W]
+        banks[3][1] = full_banks[2][1][:, W : 2 * W]
 
         nc.gpsimd.memset(w_planes[:].bitcast(I32), 0)
 
@@ -74,6 +89,9 @@ def tile_picked_place_lin_none_sub_l_kernel(tc, xT, w_words, w_scales, gate, off
             rows = slice(q * QUAD, (q + 1) * QUAD)
             nc.vector.tensor_tensor(identity[rows, rows], ramp[rows, :], ramp_t[rows, :], ALU.is_equal)
 
+        def columns(first_stage, count=1):
+            return slice(ORDER[first_stage] * W, (ORDER[first_stage] + count) * W)
+
         def load_gate(queue):
             queue.dma_start(gate_cols[:], gate[0].rearrange("(n e) -> n e", e=GATE_RUN))
 
@@ -83,23 +101,25 @@ def tile_picked_place_lin_none_sub_l_kernel(tc, xT, w_words, w_scales, gate, off
         def load_scales(queue, q):
             queue.dma_start(w_planes[QUAD * q : QUAD * q + SCALE_ROWS * PASSES, :].bitcast(I32), scale_rows[q])
 
-        def load_x(c, a):
-            nc.sync.dma_start(raws[c][a][:], x_rows[a][:, :, c * W : (c + 1) * W])
+        def load_wide(a):
+            nc.sync.dma_start(wide[a][:], x_rows[a][:, :, columns(0, 2)])
+
+        def load_x(s, a):
+            nc.sync.dma_start(raws[s][a], x_rows[a][:, :, columns(s)])
 
         load_gate(nc.sync)
-        load_x(0, 0)
+        load_wide(0)
         load_scales(nc.sync, 0)
+        load_wide(1)
+        load_w()
         load_scales(nc.sync, 1)
-        load_x(0, 1)
         load_scales(nc.sync, 2)
         load_scales(nc.sync, 3)
-        load_w()
-        load_x(1, 0)
+        load_x(2, 0)
         nc.sync.dma_start(offsets[:], offs)
-        load_x(1, 1)
-        for c in range(2, CHUNKS):
-            for a in range(PASSES):
-                load_x(c, a)
+        load_x(2, 1)
+        load_x(3, 0)
+        load_x(3, 1)
 
         halves = [windows[h][:, u * S : (u + 1) * S] for h in range(GROUPS) for u in range(T // S)]
         for half in halves[:-1]:
@@ -110,52 +130,90 @@ def tile_picked_place_lin_none_sub_l_kernel(tc, xT, w_words, w_scales, gate, off
             nc.tensor.transpose(gate_bank[:, e, :], gate_cols[:, e : e + 1].to_broadcast([P, P]), identity[:])
         nc.scalar.copy(gate_all[:].rearrange("p (n e) -> p n e", e=GATE_RUN), gate_bank.rearrange("p e n -> p n e"))
 
-        def pack(copy, c, a, lo=0, hi=W):
-            dst = grouped[c][a][:].rearrange("p (b i t) -> p b t i", i=RUN, t=PACK)
-            src = raws[c][a][:].rearrange("p t (b i) -> p b t i", i=RUN)
+        def pack(copy, s, a, lo=0, hi=W):
+            dst = grouped[s][:, a, :].rearrange("p (b i t) -> p b t i", i=RUN, t=PACK)
+            src = raws[s][a].rearrange("p t (b i) -> p b t i", i=RUN)
             copy(dst[:, lo // RUN : hi // RUN], src[:, lo // RUN : hi // RUN])
 
-        def quantize(c, a):
-            nc.vector.quantize_mx(out=codes[c][a][:].bitcast(FP8X4), scales=planes[c][a][:], in_=grouped[c][a][:])
+        def quantize(s, a):
+            nc.vector.quantize_mx(
+                out=codes[s][:, a, :].bitcast(FP8X4), scales=planes[s][:, a, :], in_=grouped[s][:, a, :]
+            )
 
-        def multiply(c, a):
-            for h in range(GROUPS):
+        def quantize_both(s):
+            nc.vector.quantize_mx(
+                out=codes[s][:].rearrange("p a j -> p (a j)").bitcast(FP8X4),
+                scales=planes[s][:].rearrange("p a j -> p (a j)"),
+                in_=grouped[s][:].rearrange("p a j -> p (a j)"),
+            )
+
+        def multiply(s):
+            steps = [(h, a) for h in range(GROUPS) for a in range(PASSES)]
+            for h, a in steps:
                 cols = slice(h * P, (h + 1) * P)
                 nc.tensor.matmul_mx(
-                    out=banks[c][h],
+                    out=banks[s][h],
                     lhsT=w_codes[:, a, cols].bitcast(FP8X4),
                     lhsT_scale=w_planes[SCALE_ROWS * a : P, cols],
-                    rhs=codes[c][a][:].bitcast(FP8X4),
-                    rhs_scale=planes[c][a][:],
+                    rhs=codes[s][:, a, :].bitcast(FP8X4),
+                    rhs_scale=planes[s][:, a, :],
                     start=(a == 0),
                     stop=(a == PASSES - 1),
                 )
 
-        def weigh(c, h):
-            nc.vector.tensor_tensor(sums[c][h][:], banks[c][h], gate_all[:, c * W : (c + 1) * W], ALU.mult)
+        def weigh(s, h):
+            nc.vector.tensor_tensor(weighed[s][h], banks[s][h], gate_all[:, columns(s)], ALU.mult)
 
-        def target(c, h):
-            return windows[h][:].indirect(offsets[:, c * LIST_COLS : (c + 1) * LIST_COLS])
+        def weigh_both(s, dst):
+            both = full_banks[s][0][:, 0 : GROUPS * W].rearrange("p (h j) -> p h j", h=GROUPS)
+            factors = gate_all[:, columns(s)].unsqueeze(1).to_broadcast([P, GROUPS, W])
+            nc.vector.tensor_tensor(dst, both, factors, ALU.mult)
 
-        def scatter_scalar(c, h):
-            nc.scalar.activation(target(c, h), sums[c][h][:], COPY)
+        def places(h, s, count=1):
+            return windows[h][:].indirect(offsets[:, ORDER[s] * LIST_COLS : (ORDER[s] + count) * LIST_COLS])
 
-        def scatter_vector(c, h):
-            nc.vector.tensor_copy(target(c, h), sums[c][h][:])
+        def scatter_scalar(s, h):
+            nc.scalar.activation(places(h, s), weighed[s][h], COPY)
+
+        def scatter_vector(s, h):
+            nc.vector.tensor_copy(places(h, s), weighed[s][h])
 
         def store(h):
             nc.sync.dma_start(out[h * P : (h + 1) * P, :], windows[h][:])
 
-        for c in range(CHUNKS):
-            for a in range(PASSES):
-                pack(nc.scalar.copy if (c, a) == (1, 0) else nc.vector.tensor_copy, c, a)
-                quantize(c, a)
-                multiply(c, a)
-            for h in range(GROUPS):
-                weigh(c, h)
-                if c >= 2 and h == 0:
-                    scatter_vector(c, h)
-                else:
-                    scatter_scalar(c, h)
+        pack(nc.vector.tensor_copy, 0, 0)
+        pack(nc.vector.tensor_copy, 1, 0, 0, VECTOR_COLS[1])
+        pack(nc.scalar.copy, 1, 0, VECTOR_COLS[1], W)
+        quantize(0, 0)
+        for s in range(2):
+            pack(nc.vector.tensor_copy, s, 1, 0, VECTOR_COLS[s])
+            pack(nc.scalar.copy, s, 1, VECTOR_COLS[s], W)
+        quantize(0, 1)
+        multiply(0)
+        quantize_both(1)
+        multiply(1)
+        pack(nc.scalar.copy, 2, 0)
         for h in range(GROUPS):
-            store(h)
+            weigh(0, h)
+            scatter_scalar(0, h)
+        pack(nc.vector.tensor_copy, 2, 1, 0, HALF)
+        pack(nc.vector.tensor_copy, 2, 1, HALF, W)
+        weigh_both(1, padded[2][:, 0:GROUPS, 0:W])
+        scatter_scalar(1, 0)
+        scatter_scalar(1, 1)
+        quantize_both(2)
+        multiply(2)
+        pack(nc.vector.tensor_copy, 3, 0)
+        quantize(3, 0)
+        pack(nc.vector.tensor_copy, 3, 1, 0, HALF)
+        pack(nc.vector.tensor_copy, 3, 1, HALF, W)
+        weigh(2, 0)
+        quantize(3, 1)
+        multiply(3)
+        scatter_vector(2, 0)
+        weigh(3, 0)
+        nc.vector.tensor_tensor(last1[:], full_banks[2][1][:, 0 : 2 * W], gate_all[:, columns(2, 2)], ALU.mult)
+        scatter_vector(3, 0)
+        store(0)
+        nc.scalar.activation(places(1, 2, 2), last1[:], COPY)
+        store(1)

@@ -36,7 +36,7 @@ def tile_picked_place_lin_none_sub_l_kernel(tc, xT, w_words, w_scales, gate, off
     nc = tc.nc
     x_rows = xT.rearrange("(a p t) j -> a p t j", a=PASSES, t=PACK)
     w_rows = w_words.rearrange("a p m r -> p a (m r)").bitcast(I32)
-    scale_rows = w_scales.rearrange("a (q i) m -> q a i m", i=SCALE_ROWS).bitcast(I32)
+    scale_rows = w_scales.rearrange("a (q i) m -> i q a m", i=SCALE_ROWS).bitcast(I32)
 
     with ExitStack() as ctx:
         keep = ctx.enter_context(tc.tile_pool(name="keep", bufs=1))
@@ -44,16 +44,17 @@ def tile_picked_place_lin_none_sub_l_kernel(tc, xT, w_words, w_scales, gate, off
 
         offsets = keep.tile([P, S // 16], U16, name="offsets")
         w_codes = keep.tile([P, PASSES, N], U32, name="w_codes", align_bytes=64)
-        w_planes = keep.tile([P, N], U8, name="w_planes", align_bytes=64)
+        w_planes = keep.tile([P, PASSES, N], U8, name="w_planes", align_bytes=64)
         windows = [keep.tile([P, T], F32, name=f"window{h}") for h in range(GROUPS)]
         grouped = [keep.tile([P, PASSES, W * PACK], BF16, name=f"grouped{s}", align_bytes=64) for s in range(CHUNKS)]
         codes = [keep.tile([P, PASSES, W], U32, name=f"codes{s}", align_bytes=64) for s in range(CHUNKS)]
         planes = [keep.tile([P, PASSES, W], U8, name=f"planes{s}", align_bytes=64) for s in range(CHUNKS)]
         wide = [keep.tile([P, PACK, 2 * W], F32, name=f"wide{a}") for a in range(PASSES)]
         plain = {s: keep.tile([P, PACK, W], F32, name=f"plain{s}") for s in (2, 3)}
-        padded = {s: keep.tile([P, PACK, HALF + W], F32, name=f"padded{s}") for s in (2, 3)}
+        padded = {s: keep.tile([P, 2 * (HALF + PACK * W)], F32, name=f"padded{s}") for s in (2, 3)}
+        pairs = {s: padded[s][:].rearrange("p (h j) -> p h j", h=GROUPS)[:, :, 0:W] for s in (2, 3)}
         raws = [[wide[a][:, :, s * W : (s + 1) * W] for a in range(PASSES)] for s in range(2)]
-        raws = raws + [[plain[s][:], padded[s][:, :, HALF:]] for s in (2, 3)]
+        raws = raws + [[plain[s][:], padded[s][:, HALF : HALF + PACK * W].rearrange("p (t j) -> p t j", t=PACK)] for s in (2, 3)]
         gate_cols = keep.tile([P, GATE_RUN], F32, name="gate_cols")
         gate_all = keep.tile([P, S], F32, name="gate_all")
         ones = keep.tile([P, QUAD], F32, name="ones")
@@ -72,14 +73,14 @@ def tile_picked_place_lin_none_sub_l_kernel(tc, xT, w_words, w_scales, gate, off
         last1 = keep.tile([P, 2 * W], F32, name="last1")
         weighed = [
             [first[:, 0, :], first[:, 1, :]],
-            [padded[2][:, 0, 0:W], padded[2][:, 1, 0:W]],
-            [padded[3][:, 0, 0:W], last1[:, 0:W]],
+            [pairs[2][:, 0, :], pairs[2][:, 1, :]],
+            [pairs[3][:, 0, :], last1[:, 0:W]],
             [last0[:], last1[:, W : 2 * W]],
         ]
         banks[2][1] = full_banks[2][1][:, 0:W]
         banks[3][1] = full_banks[2][1][:, W : 2 * W]
 
-        nc.gpsimd.memset(w_planes[:].bitcast(I32), 0)
+        nc.vector.memset(w_planes[:].bitcast(I32), 0)
 
         nc.vector.memset(ones[:], 1.0)
         nc.vector.memset(identity[:], 0.0)
@@ -99,7 +100,7 @@ def tile_picked_place_lin_none_sub_l_kernel(tc, xT, w_words, w_scales, gate, off
             nc.sync.dma_start(w_codes[:].bitcast(I32), w_rows)
 
         def load_scales(queue, q):
-            queue.dma_start(w_planes[QUAD * q : QUAD * q + SCALE_ROWS * PASSES, :].bitcast(I32), scale_rows[q])
+            queue.dma_start(w_planes[q:P:QUAD].bitcast(I32), scale_rows[q])
 
         def load_wide(a):
             nc.sync.dma_start(wide[a][:], x_rows[a][:, :, columns(0, 2)])
@@ -154,7 +155,7 @@ def tile_picked_place_lin_none_sub_l_kernel(tc, xT, w_words, w_scales, gate, off
                 nc.tensor.matmul_mx(
                     out=banks[s][h],
                     lhsT=w_codes[:, a, cols].bitcast(FP8X4),
-                    lhsT_scale=w_planes[SCALE_ROWS * a : P, cols],
+                    lhsT_scale=w_planes[:, a, cols],
                     rhs=codes[s][:, a, :].bitcast(FP8X4),
                     rhs_scale=planes[s][:, a, :],
                     start=(a == 0),
@@ -198,7 +199,7 @@ def tile_picked_place_lin_none_sub_l_kernel(tc, xT, w_words, w_scales, gate, off
             scatter_scalar(0, h)
         pack(nc.vector.tensor_copy, 2, 1, 0, HALF)
         pack(nc.vector.tensor_copy, 2, 1, HALF, W)
-        weigh_both(1, padded[2][:, 0:GROUPS, 0:W])
+        weigh_both(1, pairs[2])
         scatter_scalar(1, 0)
         scatter_scalar(1, 1)
         quantize_both(2)

@@ -28,8 +28,9 @@ SCALE_ROWS = 4
 GATE_RUN = S // P
 RUN = 4
 HALF = W // 2
+SEAM = 16
 ORDER = (0, 1, 2, 3)
-VECTOR_COLS = (80, 48)
+VECTOR_COLS = (80, 88)
 
 
 def tile_picked_place_lin_none_sub_l_kernel(tc, xT, w_words, w_scales, gate, offs, out):
@@ -50,11 +51,14 @@ def tile_picked_place_lin_none_sub_l_kernel(tc, xT, w_words, w_scales, gate, off
         codes = [keep.tile([P, PASSES, W], U32, name=f"codes{s}", align_bytes=64) for s in range(CHUNKS)]
         planes = [keep.tile([P, PASSES, W], U8, name=f"planes{s}", align_bytes=64) for s in range(CHUNKS)]
         wide = [keep.tile([P, PACK, 2 * W], F32, name=f"wide{a}") for a in range(PASSES)]
-        plain = {s: keep.tile([P, PACK, W], F32, name=f"plain{s}") for s in (2, 3)}
-        padded = {s: keep.tile([P, 2 * (HALF + PACK * W)], F32, name=f"padded{s}") for s in (2, 3)}
-        pairs = {s: padded[s][:].rearrange("p (h j) -> p h j", h=GROUPS)[:, :, 0:W] for s in (2, 3)}
+        plain = keep.tile([P, PACK, W], F32, name="plain")
+        front = 2 * W - HALF
+        padded = keep.tile([P, front + PACK * W], F32, name="padded")
+        pitch = PACK * W + W - SEAM
+        tail = keep.tile([P, pitch + PACK * W], F32, name="tail")
         raws = [[wide[a][:, :, s * W : (s + 1) * W] for a in range(PASSES)] for s in range(2)]
-        raws = raws + [[plain[s][:], padded[s][:, HALF : HALF + PACK * W].rearrange("p (t j) -> p t j", t=PACK)] for s in (2, 3)]
+        raws.append([plain[:], padded[:, front:].rearrange("p (t j) -> p t j", t=PACK)])
+        raws.append([tail[:, a * pitch : a * pitch + PACK * W].rearrange("p (t j) -> p t j", t=PACK) for a in range(PASSES)])
         gate_cols = keep.tile([P, GATE_RUN], F32, name="gate_cols")
         gate_all = keep.tile([P, S], F32, name="gate_all")
         ones = keep.tile([P, QUAD], F32, name="ones")
@@ -63,22 +67,13 @@ def tile_picked_place_lin_none_sub_l_kernel(tc, xT, w_words, w_scales, gate, off
         identity = keep.tile([P, P], F32, name="identity")
         full_banks = [[psum.tile([P, S], F32, name=f"bank{s}_{h}") for h in range(GROUPS)] for s in range(CHUNKS)]
         gate_bank = full_banks[CHUNKS - 1][GROUPS - 1][:].rearrange("p (e n) -> p e n", e=GATE_RUN)
-        joint = (1,)
-        banks = [
-            [full_banks[s][0][:, h * W : (h + 1) * W] if s in joint else full_banks[s][h][:, 0:W] for h in range(GROUPS)]
-            for s in range(CHUNKS)
-        ]
-        first = keep.tile([P, GROUPS, W], F32, name="first")
+        banks = [[full_banks[0][h][:, s * W : (s + 1) * W] for h in range(GROUPS)] for s in range(2)]
+        banks = banks + [[full_banks[s][0][:, 0:W], full_banks[2][1][:, (s - 2) * W : (s - 1) * W]] for s in (2, 3)]
+        first0 = keep.tile([P, 2 * W], F32, name="first0")
+        first1 = padded[:, 0 : 2 * W]
+        middle0 = tail[:, PACK * W : PACK * W + W]
         last0 = keep.tile([P, W], F32, name="last0")
         last1 = keep.tile([P, 2 * W], F32, name="last1")
-        weighed = [
-            [first[:, 0, :], first[:, 1, :]],
-            [pairs[2][:, 0, :], pairs[2][:, 1, :]],
-            [pairs[3][:, 0, :], last1[:, 0:W]],
-            [last0[:], last1[:, W : 2 * W]],
-        ]
-        banks[2][1] = full_banks[2][1][:, 0:W]
-        banks[3][1] = full_banks[2][1][:, W : 2 * W]
 
         nc.vector.memset(w_planes[:].bitcast(I32), 0)
 
@@ -136,85 +131,78 @@ def tile_picked_place_lin_none_sub_l_kernel(tc, xT, w_words, w_scales, gate, off
             src = raws[s][a].rearrange("p t (b i) -> p b t i", i=RUN)
             copy(dst[:, lo // RUN : hi // RUN], src[:, lo // RUN : hi // RUN])
 
+        def pack_seam():
+            dst = grouped[3][:].rearrange("p a c -> p (a c)")[:, (W - SEAM) * PACK : (W + SEAM) * PACK]
+            src = tail[:, W - SEAM : W - SEAM + PASSES * PACK * W].rearrange("p (a t j) -> p a t j", a=PASSES, t=PACK)
+            nc.vector.tensor_copy(
+                dst.rearrange("p (a b i t) -> p a b t i", a=PASSES, i=RUN, t=PACK),
+                src[:, :, :, 0:SEAM].rearrange("p a t (b i) -> p a b t i", i=RUN),
+            )
+
         def quantize(s, a):
             nc.vector.quantize_mx(
                 out=codes[s][:, a, :].bitcast(FP8X4), scales=planes[s][:, a, :], in_=grouped[s][:, a, :]
             )
 
-        def quantize_both(s):
-            nc.vector.quantize_mx(
-                out=codes[s][:].rearrange("p a j -> p (a j)").bitcast(FP8X4),
-                scales=planes[s][:].rearrange("p a j -> p (a j)"),
-                in_=grouped[s][:].rearrange("p a j -> p (a j)"),
+        def multiply(s, h, a):
+            cols = slice(h * P, (h + 1) * P)
+            nc.tensor.matmul_mx(
+                out=banks[s][h],
+                lhsT=w_codes[:, a, cols].bitcast(FP8X4),
+                lhsT_scale=w_planes[:, a, cols],
+                rhs=codes[s][:, a, :].bitcast(FP8X4),
+                rhs_scale=planes[s][:, a, :],
+                start=(a == 0),
+                stop=(a == PASSES - 1),
             )
 
-        def multiply(s):
-            steps = [(h, a) for h in range(GROUPS) for a in range(PASSES)]
-            for h, a in steps:
-                cols = slice(h * P, (h + 1) * P)
-                nc.tensor.matmul_mx(
-                    out=banks[s][h],
-                    lhsT=w_codes[:, a, cols].bitcast(FP8X4),
-                    lhsT_scale=w_planes[:, a, cols],
-                    rhs=codes[s][:, a, :].bitcast(FP8X4),
-                    rhs_scale=planes[s][:, a, :],
-                    start=(a == 0),
-                    stop=(a == PASSES - 1),
-                )
-
-        def weigh(s, h):
-            nc.vector.tensor_tensor(weighed[s][h], banks[s][h], gate_all[:, columns(s)], ALU.mult)
-
-        def weigh_both(s, dst):
-            both = full_banks[s][0][:, 0 : GROUPS * W].rearrange("p (h j) -> p h j", h=GROUPS)
-            factors = gate_all[:, columns(s)].unsqueeze(1).to_broadcast([P, GROUPS, W])
-            nc.vector.tensor_tensor(dst, both, factors, ALU.mult)
+        def weigh(dst, bank, s, count=1):
+            nc.vector.tensor_tensor(dst, bank[:, 0 : count * W], gate_all[:, columns(s, count)], ALU.mult)
 
         def places(h, s, count=1):
             return windows[h][:].indirect(offsets[:, ORDER[s] * LIST_COLS : (ORDER[s] + count) * LIST_COLS])
 
-        def scatter_scalar(s, h):
-            nc.scalar.activation(places(h, s), weighed[s][h], COPY)
-
-        def scatter_vector(s, h):
-            nc.vector.tensor_copy(places(h, s), weighed[s][h])
-
         def store(h):
             nc.sync.dma_start(out[h * P : (h + 1) * P, :], windows[h][:])
 
-        pack(nc.vector.tensor_copy, 0, 0)
-        pack(nc.vector.tensor_copy, 1, 0, 0, VECTOR_COLS[1])
-        pack(nc.scalar.copy, 1, 0, VECTOR_COLS[1], W)
-        quantize(0, 0)
+        for s in range(2):
+            pack(nc.vector.tensor_copy, s, 0)
+        for s in range(2):
+            quantize(s, 0)
         for s in range(2):
             pack(nc.vector.tensor_copy, s, 1, 0, VECTOR_COLS[s])
             pack(nc.scalar.copy, s, 1, VECTOR_COLS[s], W)
-        quantize(0, 1)
-        multiply(0)
-        quantize_both(1)
-        multiply(1)
-        pack(nc.scalar.copy, 2, 0)
+        for s in range(2):
+            quantize(s, 1)
         for h in range(GROUPS):
-            weigh(0, h)
-            scatter_scalar(0, h)
+            for s in range(2):
+                for a in range(PASSES):
+                    multiply(s, h, a)
+        pack(nc.scalar.copy, 2, 0)
+        weigh(first0[:], full_banks[0][0], 0, 2)
+        nc.scalar.activation(places(0, 0, 2), first0[:], COPY)
+        quantize(2, 0)
         pack(nc.vector.tensor_copy, 2, 1, 0, HALF)
         pack(nc.vector.tensor_copy, 2, 1, HALF, W)
-        weigh_both(1, pairs[2])
-        scatter_scalar(1, 0)
-        scatter_scalar(1, 1)
-        quantize_both(2)
-        multiply(2)
-        pack(nc.vector.tensor_copy, 3, 0)
+        weigh(first1, full_banks[0][1], 0, 2)
+        nc.scalar.activation(places(1, 0, 2), first1, COPY)
+        quantize(2, 1)
+        for a in range(PASSES):
+            for h in range(GROUPS):
+                multiply(2, h, a)
+        pack(nc.vector.tensor_copy, 3, 0, 0, W - SEAM)
+        pack_seam()
+        pack(nc.vector.tensor_copy, 3, 1, SEAM, W)
         quantize(3, 0)
-        pack(nc.vector.tensor_copy, 3, 1, 0, HALF)
-        pack(nc.vector.tensor_copy, 3, 1, HALF, W)
-        weigh(2, 0)
+        weigh(middle0, full_banks[2][0], 2)
         quantize(3, 1)
-        multiply(3)
-        scatter_vector(2, 0)
-        weigh(3, 0)
-        nc.vector.tensor_tensor(last1[:], full_banks[2][1][:, 0 : 2 * W], gate_all[:, columns(2, 2)], ALU.mult)
-        scatter_vector(3, 0)
+        for a in range(PASSES):
+            for h in range(GROUPS):
+                multiply(3, h, a)
+        nc.vector.tensor_copy(places(0, 2), middle0)
+        weigh(last0[:], full_banks[3][0], 3)
+        weigh(last1[:], full_banks[2][1], 2, 2)
+        nc.vector.tensor_copy(places(0, 3), last0[:])
         store(0)
         nc.scalar.activation(places(1, 2, 2), last1[:], COPY)
         store(1)

@@ -27,7 +27,6 @@ QUADS = P // QUAD
 SCALE_ROWS = 4
 GATE_RUN = S // P
 RUN = 4
-HALF = W // 2
 SEAM = 16
 ORDER = (0, 1, 2, 3)
 VECTOR_COLS = (80, 88)
@@ -51,14 +50,12 @@ def tile_picked_place_lin_none_sub_l_kernel(tc, xT, w_words, w_scales, gate, off
         codes = [keep.tile([P, PASSES, W], U32, name=f"codes{s}", align_bytes=64) for s in range(CHUNKS)]
         planes = [keep.tile([P, PASSES, W], U8, name=f"planes{s}", align_bytes=64) for s in range(CHUNKS)]
         wide = [keep.tile([P, PACK, 2 * W], F32, name=f"wide{a}") for a in range(PASSES)]
-        plain = keep.tile([P, PACK, W], F32, name="plain")
-        front = 2 * W - HALF
-        padded = keep.tile([P, front + PACK * W], F32, name="padded")
         pitch = PACK * W + W - SEAM
-        tail = keep.tile([P, pitch + PACK * W], F32, name="tail")
+        seamed = keep.tile([P, pitch + PACK * W], F32, name="seamed")
+        plain = [keep.tile([P, PACK, W], F32, name=f"plain{a}") for a in range(PASSES)]
         raws = [[wide[a][:, :, s * W : (s + 1) * W] for a in range(PASSES)] for s in range(2)]
-        raws.append([plain[:], padded[:, front:].rearrange("p (t j) -> p t j", t=PACK)])
-        raws.append([tail[:, a * pitch : a * pitch + PACK * W].rearrange("p (t j) -> p t j", t=PACK) for a in range(PASSES)])
+        raws.append([seamed[:, c : c + PACK * W].rearrange("p (t j) -> p t j", t=PACK) for c in (0, pitch)])
+        raws.append([plain[a][:] for a in range(PASSES)])
         gate_cols = keep.tile([P, GATE_RUN], F32, name="gate_cols")
         gate_all = keep.tile([P, S], F32, name="gate_all")
         ones = keep.tile([P, QUAD], F32, name="ones")
@@ -70,8 +67,8 @@ def tile_picked_place_lin_none_sub_l_kernel(tc, xT, w_words, w_scales, gate, off
         banks = [[full_banks[0][h][:, s * W : (s + 1) * W] for h in range(GROUPS)] for s in range(2)]
         banks = banks + [[full_banks[s][0][:, 0:W], full_banks[2][1][:, (s - 2) * W : (s - 1) * W]] for s in (2, 3)]
         first0 = keep.tile([P, 2 * W], F32, name="first0")
-        first1 = padded[:, 0 : 2 * W]
-        middle0 = tail[:, PACK * W : PACK * W + W]
+        first1 = grouped[2][:, 1, :].bitcast(F32)
+        middle0 = plain[0][:, 0, :]
         last0 = keep.tile([P, W], F32, name="last0")
         last1 = keep.tile([P, 2 * W], F32, name="last1")
 
@@ -131,9 +128,9 @@ def tile_picked_place_lin_none_sub_l_kernel(tc, xT, w_words, w_scales, gate, off
             src = raws[s][a].rearrange("p t (b i) -> p b t i", i=RUN)
             copy(dst[:, lo // RUN : hi // RUN], src[:, lo // RUN : hi // RUN])
 
-        def pack_seam():
-            dst = grouped[3][:].rearrange("p a c -> p (a c)")[:, (W - SEAM) * PACK : (W + SEAM) * PACK]
-            src = tail[:, W - SEAM : W - SEAM + PASSES * PACK * W].rearrange("p (a t j) -> p a t j", a=PASSES, t=PACK)
+        def pack_seam(s):
+            dst = grouped[s][:].rearrange("p a c -> p (a c)")[:, (W - SEAM) * PACK : (W + SEAM) * PACK]
+            src = seamed[:, W - SEAM : W - SEAM + PASSES * PACK * W].rearrange("p (a t j) -> p a t j", a=PASSES, t=PACK)
             nc.vector.tensor_copy(
                 dst.rearrange("p (a b i t) -> p a b t i", a=PASSES, i=RUN, t=PACK),
                 src[:, :, :, 0:SEAM].rearrange("p a t (b i) -> p a b t i", i=RUN),
@@ -178,22 +175,21 @@ def tile_picked_place_lin_none_sub_l_kernel(tc, xT, w_words, w_scales, gate, off
             for s in range(2):
                 for a in range(PASSES):
                     multiply(s, h, a)
-        pack(nc.scalar.copy, 2, 0)
+        pack(nc.scalar.copy, 2, 0, 0, W - SEAM)
         weigh(first0[:], full_banks[0][0], 0, 2)
         nc.scalar.activation(places(0, 0, 2), first0[:], COPY)
-        quantize(2, 0)
-        pack(nc.vector.tensor_copy, 2, 1, 0, HALF)
-        pack(nc.vector.tensor_copy, 2, 1, HALF, W)
+        pack_seam(2)
+        pack(nc.vector.tensor_copy, 2, 1, SEAM, W)
+        for a in range(PASSES):
+            quantize(2, a)
+        for h in range(GROUPS):
+            for a in range(PASSES):
+                multiply(2, h, a)
+        pack(nc.vector.tensor_copy, 3, 0)
         weigh(first1, full_banks[0][1], 0, 2)
         nc.scalar.activation(places(1, 0, 2), first1, COPY)
-        quantize(2, 1)
-        for a in range(PASSES):
-            for h in range(GROUPS):
-                multiply(2, h, a)
-        pack(nc.vector.tensor_copy, 3, 0, 0, W - SEAM)
-        pack_seam()
-        pack(nc.vector.tensor_copy, 3, 1, SEAM, W)
         quantize(3, 0)
+        pack(nc.vector.tensor_copy, 3, 1)
         weigh(middle0, full_banks[2][0], 2)
         quantize(3, 1)
         for a in range(PASSES):

@@ -26,7 +26,7 @@ QUAD = 32
 QUADS = P // QUAD
 SCALE_ROWS = 4
 GATE_RUN = S // P
-RUN = 4
+RUN = 2
 SEAM = 16
 ORDER = (0, 1, 2, 3)
 VECTOR_COLS = (80, 88)

@@ -57,7 +57,7 @@ def tile_picked_place_lin_none_sub_l_kernel(tc, xT, w_words, w_scales, gate, off
         raws.append([seamed[:, c : c + PACK * W].rearrange("p (t j) -> p t j", t=PACK) for c in (0, pitch)])
         raws.append([plain[a][:] for a in range(PASSES)])
         gate_cols = keep.tile([P, GATE_RUN], F32, name="gate_cols")
-        gate_all = keep.tile([P, S], F32, name="gate_all")
+        gate_all = wide[1][:, 0:2, :].rearrange("p t j -> p (t j)")
         ones = keep.tile([P, QUAD], F32, name="ones")
         ramp = keep.tile([P, QUAD], F32, name="ramp", align_bytes=64)
         ramp_t = keep.tile([P, QUAD], F32, name="ramp_t", align_bytes=64)
@@ -100,8 +100,8 @@ def tile_picked_place_lin_none_sub_l_kernel(tc, xT, w_words, w_scales, gate, off
         def load_x(s, a):
             nc.sync.dma_start(raws[s][a], x_rows[a][:, :, columns(s)])
 
-        load_gate(nc.sync)
         load_wide(0)
+        load_gate(nc.sync)
         load_scales(nc.sync, 0)
         load_wide(1)
         load_w()
@@ -121,7 +121,6 @@ def tile_picked_place_lin_none_sub_l_kernel(tc, xT, w_words, w_scales, gate, off
 
         for e in range(GATE_RUN):
             nc.tensor.transpose(gate_bank[:, e, :], gate_cols[:, e : e + 1].to_broadcast([P, P]), identity[:])
-        nc.scalar.copy(gate_all[:].rearrange("p (n e) -> p n e", e=GATE_RUN), gate_bank.rearrange("p e n -> p n e"))
 
         def pack(copy, s, a, lo=0, hi=W):
             dst = grouped[s][:, a, :].rearrange("p (b i t) -> p b t i", i=RUN, t=PACK)
@@ -169,6 +168,7 @@ def tile_picked_place_lin_none_sub_l_kernel(tc, xT, w_words, w_scales, gate, off
         for s in range(2):
             pack(nc.vector.tensor_copy, s, 1, 0, VECTOR_COLS[s])
             pack(nc.scalar.copy, s, 1, VECTOR_COLS[s], W)
+        nc.scalar.copy(gate_all.rearrange("p (n e) -> p n e", e=GATE_RUN), gate_bank.rearrange("p e n -> p n e"))
         for s in range(2):
             quantize(s, 1)
         for h in range(GROUPS):

@@ -74,7 +74,7 @@ def tile_picked_place_lin_none_sub_l_kernel(tc, xT, w_words, w_scales, gate, off
 
         nc.vector.memset(w_planes[:].bitcast(I32), 0)
 
-        nc.vector.memset(ones[:], 1.0)
+        nc.gpsimd.memset(ones[:], 1.0)
         nc.vector.memset(identity[:], 0.0)
         nc.vector.tensor_tensor_scan(ramp[:], ones[:], ones[:], 0.0, ALU.mult, ALU.add)
         nc.vector.transpose(ramp_t[:], ramp[:])
@@ -114,10 +114,9 @@ def tile_picked_place_lin_none_sub_l_kernel(tc, xT, w_words, w_scales, gate, off
         load_x(3, 0)
         load_x(3, 1)
 
-        halves = [windows[h][:, u * S : (u + 1) * S] for h in range(GROUPS) for u in range(T // S)]
-        for half in halves[:-1]:
-            nc.vector.memset(half, 0.0)
-        nc.scalar.activation(halves[-1], halves[0], COPY)
+        nc.vector.memset(windows[0][:], 0.0)
+        nc.vector.memset(windows[1][:, 0:S], 0.0)
+        nc.scalar.activation(windows[1][:, S:T], windows[0][:, 0:S], COPY)
 
         for e in range(GATE_RUN):
             nc.tensor.transpose(gate_bank[:, e, :], gate_cols[:, e : e + 1].to_broadcast([P, P]), identity[:])

from contextlib import ExitStack

import concourse.mybir as mybir

K, T, S, N = 1024, 1024, 512, 256
FLOPS = 2 * K * S * N

F32 = mybir.dt.float32
BF16 = mybir.dt.bfloat16
I32 = mybir.dt.int32
U32 = mybir.dt.uint32
U16 = mybir.dt.uint16
U8 = mybir.dt.uint8
FP8X4 = mybir.dt.float8_e4m3fn_x4
ALU = mybir.AluOpType
COPY = mybir.ActivationFunctionType.Copy

P = 128
PACK = 4
PASSES = K // (P * PACK)
GROUPS = N // P
W = 128
CHUNKS = S // W
LIST_COLS = W // 16
QUAD = 32
QUADS = P // QUAD
SCALE_ROWS = 4
GATE_RUN = S // P
RUN = 2
SEAM = 16
ORDER = (0, 1, 2, 3)
VECTOR_COLS = (80, 88)


def tile_picked_place_lin_none_sub_l_kernel(tc, xT, w_words, w_scales, gate, offs, out):
    nc = tc.nc
    x_rows = xT.rearrange("(a p t) j -> a p t j", a=PASSES, t=PACK)
    w_rows = w_words.rearrange("a p m r -> p a (m r)").bitcast(I32)
    scale_rows = w_scales.rearrange("a (q i) m -> i q a m", i=SCALE_ROWS).bitcast(I32)

    with ExitStack() as ctx:
        keep = ctx.enter_context(tc.tile_pool(name="keep", bufs=1))
        psum = ctx.enter_context(tc.psum_pool(name="psum", bufs=1))

        offsets = keep.tile([P, S // 16], U16, name="offsets")
        w_codes = keep.tile([P, PASSES, N], U32, name="w_codes", align_bytes=64)
        w_planes = keep.tile([P, PASSES, N], U8, name="w_planes", align_bytes=64)
        windows = [keep.tile([P, T], F32, name=f"window{h}") for h in range(GROUPS)]
        grouped = [keep.tile([P, PASSES, W * PACK], BF16, name=f"grouped{s}", align_bytes=64) for s in range(CHUNKS)]
        codes = [keep.tile([P, PASSES, W], U32, name=f"codes{s}", align_bytes=64) for s in range(CHUNKS)]
        planes = [keep.tile([P, PASSES, W], U8, name=f"planes{s}", align_bytes=64) for s in range(CHUNKS)]
        wide = [keep.tile([P, PACK, 2 * W], F32, name=f"wide{a}") for a in range(PASSES)]
        pitch = PACK * W + W - SEAM
        seamed = keep.tile([P, pitch + PACK * W], F32, name="seamed")
        plain = [keep.tile([P, PACK, W], F32, name=f"plain{a}") for a in range(PASSES)]
        raws = [[wide[a][:, :, s * W : (s + 1) * W] for a in range(PASSES)] for s in range(2)]
        raws.append([seamed[:, c : c + PACK * W].rearrange("p (t j) -> p t j", t=PACK) for c in (0, pitch)])
        raws.append([plain[a][:] for a in range(PASSES)])
        gate_cols = keep.tile([P, GATE_RUN], F32, name="gate_cols")
        gate_all = wide[1][:, 0:2, :].rearrange("p t j -> p (t j)")
        ones = keep.tile([P, QUAD], F32, name="ones")
        ramp = keep.tile([P, QUAD], F32, name="ramp", align_bytes=64)
        ramp_t = keep.tile([P, QUAD], F32, name="ramp_t", align_bytes=64)
        identity = keep.tile([P, P], F32, name="identity")
        full_banks = [[psum.tile([P, S], F32, name=f"bank{s}_{h}") for h in range(GROUPS)] for s in range(CHUNKS)]
        gate_bank = full_banks[CHUNKS - 1][GROUPS - 1][:].rearrange("p (e n) -> p e n", e=GATE_RUN)
        banks = [[full_banks[0][h][:, s * W : (s + 1) * W] for h in range(GROUPS)] for s in range(2)]
        banks = banks + [[full_banks[s][0][:, 0:W], full_banks[2][1][:, (s - 2) * W : (s - 1) * W]] for s in (2, 3)]
        first0 = keep.tile([P, 2 * W], F32, name="first0")
        first1 = grouped[2][:, 1, :].bitcast(F32)
        middle0 = plain[0][:, 0, :]
        last0 = keep.tile([P, W], F32, name="last0")
        last1 = keep.tile([P, 2 * W], F32, name="last1")

        nc.vector.memset(w_planes[:].bitcast(I32), 0)

        nc.gpsimd.memset(ones[:], 1.0)
        nc.vector.memset(identity[:], 0.0)
        nc.vector.tensor_tensor_scan(ramp[:], ones[:], ones[:], 0.0, ALU.mult, ALU.add)
        nc.vector.transpose(ramp_t[:], ramp[:])
        for q in range(QUADS):
            rows = slice(q * QUAD, (q + 1) * QUAD)
            nc.vector.tensor_tensor(identity[rows, rows], ramp[rows, :], ramp_t[rows, :], ALU.is_equal)

        def columns(first_stage, count=1):
            return slice(ORDER[first_stage] * W, (ORDER[first_stage] + count) * W)

        def load_gate(queue):
            queue.dma_start(gate_cols[:], gate[0].rearrange("(n e) -> n e", e=GATE_RUN))

        def load_w():
            nc.sync.dma_start(w_codes[:].bitcast(I32), w_rows)

        def load_scales(queue, q):
            queue.dma_start(w_planes[q:P:QUAD].bitcast(I32), scale_rows[q])

        def load_wide(a):
            nc.sync.dma_start(wide[a][:], x_rows[a][:, :, columns(0, 2)])

        def load_x(s, a):
            nc.sync.dma_start(raws[s][a], x_rows[a][:, :, columns(s)])

        load_wide(0)
        load_gate(nc.sync)
        load_scales(nc.sync, 0)
        load_wide(1)
        load_w()
        load_scales(nc.sync, 1)
        load_scales(nc.sync, 2)
        load_scales(nc.sync, 3)
        load_x(2, 0)
        nc.sync.dma_start(offsets[:], offs)
        load_x(2, 1)
        load_x(3, 0)
        load_x(3, 1)

        nc.vector.memset(windows[0][:], 0.0)
        nc.vector.memset(windows[1][:, 0:S], 0.0)
        nc.scalar.activation(windows[1][:, S:T], windows[0][:, 0:S], COPY)

        for e in range(GATE_RUN):
            nc.tensor.transpose(gate_bank[:, e, :], gate_cols[:, e : e + 1].to_broadcast([P, P]), identity[:])

        def pack(copy, s, a, lo=0, hi=W):
            dst = grouped[s][:, a, :].rearrange("p (b i t) -> p b t i", i=RUN, t=PACK)
            src = raws[s][a].rearrange("p t (b i) -> p b t i", i=RUN)
            copy(dst[:, lo // RUN : hi // RUN], src[:, lo // RUN : hi // RUN])

        def pack_seam(s):
            dst = grouped[s][:].rearrange("p a c -> p (a c)")[:, (W - SEAM) * PACK : (W + SEAM) * PACK]
            src = seamed[:, W - SEAM : W - SEAM + PASSES * PACK * W].rearrange("p (a t j) -> p a t j", a=PASSES, t=PACK)
            nc.vector.tensor_copy(
                dst.rearrange("p (a b i t) -> p a b t i", a=PASSES, i=RUN, t=PACK),
                src[:, :, :, 0:SEAM].rearrange("p a t (b i) -> p a b t i", i=RUN),
            )

        def quantize(s, a):
            nc.vector.quantize_mx(
                out=codes[s][:, a, :].bitcast(FP8X4), scales=planes[s][:, a, :], in_=grouped[s][:, a, :]
            )

        def multiply(s, h, a):
            cols = slice(h * P, (h + 1) * P)
            nc.tensor.matmul_mx(
                out=banks[s][h],
                lhsT=w_codes[:, a, cols].bitcast(FP8X4),
                lhsT_scale=w_planes[:, a, cols],
                rhs=codes[s][:, a, :].bitcast(FP8X4),
                rhs_scale=planes[s][:, a, :],
                start=(a == 0),
                stop=(a == PASSES - 1),
            )

        def weigh(dst, bank, s, count=1):
            nc.vector.tensor_tensor(dst, bank[:, 0 : count * W], gate_all[:, columns(s, count)], ALU.mult)

        def places(h, s, count=1):
            return windows[h][:].indirect(offsets[:, ORDER[s] * LIST_COLS : (ORDER[s] + count) * LIST_COLS])

        def store(h):
            nc.sync.dma_start(out[h * P : (h + 1) * P, :], windows[h][:])

        for s in range(2):
            pack(nc.vector.tensor_copy, s, 0)
        for s in range(2):
            quantize(s, 0)
        for s in range(2):
            pack(nc.vector.tensor_copy, s, 1, 0, VECTOR_COLS[s])
            pack(nc.scalar.copy, s, 1, VECTOR_COLS[s], W)
        nc.scalar.copy(gate_all.rearrange("p (n e) -> p n e", e=GATE_RUN), gate_bank.rearrange("p e n -> p n e"))
        for s in range(2):
            quantize(s, 1)
        for h in range(GROUPS):
            for s in range(2):
                for a in range(PASSES):
                    multiply(s, h, a)
        pack(nc.scalar.copy, 2, 0, 0, W - SEAM)
        weigh(first0[:], full_banks[0][0], 0, 2)
        nc.scalar.activation(places(0, 0, 2), first0[:], COPY)
        pack_seam(2)
        pack(nc.vector.tensor_copy, 2, 1, SEAM, W)
        for a in range(PASSES):
            quantize(2, a)
        for h in range(GROUPS):
            for a in range(PASSES):
                multiply(2, h, a)
        pack(nc.vector.tensor_copy, 3, 0)
        weigh(first1, full_banks[0][1], 0, 2)
        nc.scalar.activation(places(1, 0, 2), first1, COPY)
        quantize(3, 0)
        pack(nc.vector.tensor_copy, 3, 1)
        weigh(middle0, full_banks[2][0], 2)
        quantize(3, 1)
        for a in range(PASSES):
            for h in range(GROUPS):
                multiply(3, h, a)
        nc.vector.tensor_copy(places(0, 2), middle0)
        weigh(last0[:], full_banks[3][0], 3)
        weigh(last1[:], full_banks[2][1], 2, 2)
        nc.vector.tensor_copy(places(0, 3), last0[:])
        store(0)
        nc.scalar.activation(places(1, 2, 2), last1[:], COPY)
        store(1)
